import numpy as np
import ml_dtypes


def mxq(x, axis, fmt="e4m3"):
    dtype, down = {"e4m3": (ml_dtypes.float8_e4m3fn, 7), "e5m2": (ml_dtypes.float8_e5m2, 14)}[fmt]
    v = np.moveaxis(np.asarray(x, np.float32).astype(ml_dtypes.bfloat16).astype(np.float64), axis, -1)
    blocks = v.reshape(v.shape[:-1] + (-1, 32))
    amax = np.abs(blocks).max(-1, keepdims=True)
    byte = np.maximum(np.where(amax > 0, np.frexp(amax)[1] - 1 + 127, 0) - down, 1)
    scale = np.exp2(byte - 127.0)
    codes = (blocks / scale).astype(np.float32).astype(dtype).astype(np.float64)
    return np.moveaxis((codes * scale).reshape(v.shape), -1, axis)


WIDE = False


def mx_kscale(k):
    if not WIDE:
        return np.ones(k)
    levels = np.array([10, -10, 5, -5, 0])
    if k % 512:
        return np.exp2(np.random.permutation(np.resize(levels, k // 32))).repeat(32)
    a = np.empty((k // 512, 16))
    for p in range(k // 512):
        a[p, :8] = np.random.permutation(np.resize(levels, 8))
        for g in range(8):
            far = levels[np.abs(levels - a[p, g]) >= 10]
            a[p, g + 8] = far[np.random.randint(len(far))]
    return np.exp2(a.ravel()).repeat(32)


def f64(x):
    return np.asarray(x).astype(np.float64)


def striped(idx):
    return np.tile(idx.reshape(-1, 16).T, (8, 1)).astype(np.uint16)


def unstriped(offs):
    return offs[:16].T.reshape(-1).astype(np.int64)


def striped8(idx):
    return np.concatenate([x.reshape(-1, 16).T for x in idx]).astype(np.uint16)


def runs(offs, k):
    lists = np.stack([offs[16 * r : 16 * r + 16].T.reshape(-1) for r in range(8)]).astype(np.int64)
    return lists[np.arange(k) % 512 // 64]


def pack_weight(w):
    k, n = w.shape
    w = f64(np.asarray(w, np.float32).astype(ml_dtypes.bfloat16)).reshape(k // 32, 32, n)
    amax = np.abs(w).max(1)
    byte = np.clip(np.where(amax > 0, np.frexp(amax)[1] - 1 + 127 - 7, 1), 1, 254)
    scaled = (w * np.exp2(127.0 - byte)[:, None, :]).reshape(k, n).astype(np.float32)
    words = np.ascontiguousarray(scaled.reshape(k // 512, 128, 4, n).transpose(0, 1, 3, 2)).astype(ml_dtypes.float8_e4m3fn).view(np.uint8)
    return words, np.ascontiguousarray(byte.astype(np.uint8).reshape(k // 512, 16, n))


def unpack_weight(words, scales):
    g, p, n, _ = words.shape
    vals = np.ascontiguousarray(words).view(ml_dtypes.float8_e4m3fn).astype(np.float64) * np.repeat(np.exp2(scales.astype(np.float64) - 127.0), 8, axis=1)[..., None]
    return vals.transpose(0, 1, 3, 2).reshape(g * 512, n)


def sigmoid(v):
    return 1.0 / (1.0 + np.exp(-np.maximum(v, -700.0)))


K, T, S, N, H = 512, 2048, 512, 512, 512


def setup_inputs():
    n = np.random.standard_normal
    s = mx_kscale(K)[:, None]
    u = mx_kscale(H)
    packed_xT = pack_weight(n((K, T)) * s)
    return {
        "x_words": packed_xT[0],
        "x_scales": packed_xT[1],
        "w1": (n((K, H)) / np.sqrt(K) / s).astype(np.float32),
        "gn": (np.random.uniform(0.5, 1.5, (H, 1)) * u[:, None]).astype(np.float32),
        "w2": (n((H, N)) / np.sqrt(H) / u[:, None]).astype(np.float32),
        "offs": striped(np.random.permutation(T)[:S]),
        "p1": striped8(np.stack([np.random.permutation(S) for _ in range(8)])),
        "p2": striped8(np.stack([np.random.permutation(S) for _ in range(8)])),
        "p3": striped8(np.stack([np.random.permutation(S) for _ in range(8)])),
    }


def reference(x_words, x_scales, w1, gn, w2, offs, p1, p2, p3):
    xq = unpack_weight(x_words, x_scales)[:, unstriped(offs)]
    y = np.tanh(mxq(f64(w1), 0, "e4m3").T @ xq)
    fl = y[np.arange(H)[:, None], runs(p1, H)] + y[np.arange(H)[:, None], runs(p2, H)] + y[np.arange(H)[:, None], runs(p3, H)]
    pr = sigmoid(-2.0 * (y * fl))
    z = f64(gn) * (y - (2.0 * (y * pr)))
    return mxq(f64(w2), 0, "e4m3").T @ mxq(z, 0, "e4m3")

@@ -1,0 +1,284 @@
+from contextlib import ExitStack
+
+import concourse.mybir as mybir
+
+K, T, S, N, H = 512, 2048, 512, 512, 512
+FLOPS = 2 * K * H * S + 2 * H * N * S
+
+F32 = mybir.dt.float32
+BF16 = mybir.dt.bfloat16
+I32 = mybir.dt.int32
+U32 = mybir.dt.uint32
+U16 = mybir.dt.uint16
+U8 = mybir.dt.uint8
+FP8X4 = mybir.dt.float8_e4m3fn_x4
+ALU = mybir.AluOpType
+ACT = mybir.ActivationFunctionType
+
+P = 128
+PACK = 4
+HALF = S // 2
+CHUNKS = ((0, 256), (256, 128), (384, 128))
+W1_VECTOR_COLS = 80
+BIG = 3.0e38
+RUN = 4
+
+
+def tile_picked_isingm_none_p_kernel(tc, x_words, x_scales, w1, gn, w2, offs, p1, p2, p3, out):
+    nc = tc.nc
+    with ExitStack() as ctx:
+        sb = ctx.enter_context(tc.tile_pool(name="sb", bufs=1))
+        ps = ctx.enter_context(tc.psum_pool(name="ps", bufs=1))
+
+        def alloc(name, shape, dtype):
+            return sb.tile(shape, dtype, name=name, align_bytes=64)
+
+        offs_sb = sb.tile([P, S // 16], U16, name="offs_sb")
+        lists = [sb.tile([P, S // 16], U16, name="list%d" % r) for r in range(3)]
+        xs_win = alloc("xs_win", [P, T], U8)
+        xw_win = alloc("xw_win", [P, T], I32)
+        w1_raw = alloc("w1_raw", [P, PACK, H], F32)
+        w2_raw = alloc("w2_raw", [P, PACK, N], F32)
+        gn_sb = alloc("gn_sb", [P, PACK], F32)
+        warm = alloc("warm", [P, 1], F32)
+        warm_out = alloc("warm_out", [P, 1], F32)
+
+        nc.vector.memset(xs_win[:].bitcast(I32), 0)
+        nc.gpsimd.memset(warm[:], 0.0)
+        nc.scalar.activation(warm_out[:], warm[:], ACT.Sigmoid)
+
+        nc.sync.dma_start(offs_sb[:], offs)
+        nc.sync.dma_start(w1_raw[:], w1.rearrange("(p j) c -> p j c", j=PACK))
+        for q in range(4):
+            nc.sync.dma_start(xs_win[32 * q : 32 * q + 4, :].bitcast(I32), x_scales[0, 4 * q : 4 * q + 4, :].bitcast(I32))
+        nc.sync.dma_start(gn_sb[:], gn.rearrange("(p t) o -> p (t o)", t=PACK))
+        nc.sync.dma_start(xw_win[:], x_words[0].rearrange("p n t -> p (n t)").bitcast(I32))
+        for lst, src in zip(lists, (p1, p2, p3)):
+            nc.sync.dma_start(lst[:], src)
+        nc.sync.dma_start(w2_raw[:], w2.rearrange("(p j) c -> p j c", j=PACK))
+
+        w1_bf = alloc("w1_bf", [P, PACK, P, PACK], BF16)
+        w1_src = w1_raw[:].rearrange("p j (m t) -> p m j t", t=PACK)
+        w1_dst = w1_bf[:].rearrange("p t m j -> p m j t")
+        nc.vector.tensor_copy(w1_dst[:, :W1_VECTOR_COLS], w1_src[:, :W1_VECTOR_COLS])
+        nc.scalar.copy(w1_dst[:, W1_VECTOR_COLS:], w1_src[:, W1_VECTOR_COLS:])
+
+        gain2 = alloc("gain2", [P, PACK], F32)
+        recip = alloc("recip", [P, PACK], F32)
+        recip_hi = alloc("recip_hi", [P, PACK], F32)
+        unscale = alloc("unscale", [P, PACK], F32)
+        nc.vector.tensor_scalar(gain2[:], gn_sb[:], 2.0, None, ALU.mult)
+        nc.vector.reciprocal(recip[:], gn_sb[:])
+
+        w1_codes = alloc("w1_codes", [P, H], U32)
+        w1_scales = alloc("w1_scales", [P, H], U8)
+        nc.vector.quantize_mx(w1_codes[:].bitcast(FP8X4), w1_scales[:], w1_bf[:].rearrange("p t m j -> p (t m j)"))
+        nc.vector.tensor_scalar(recip_hi[:], recip[:], 2.0, BIG, ALU.mult, ALU.min)
+
+        xs = alloc("xs", [P, S], U8)
+        nc.vector.tensor_copy(xs[:], xs_win[:].indirect(offs_sb[:]))
+        nc.vector.tensor_scalar(unscale[:], recip_hi[:], -BIG, None, ALU.max)
+
+        banks = {}
+        banks[0, 0] = ps.tile([P, HALF], F32, name="y00", tag="bankA")[:]
+        banks[0, 1] = ps.tile([P, HALF], F32, name="y01", tag="bankB")[:]
+        full = {}
+        for t in range(1, PACK):
+            full[t] = ps.tile([P, S], F32, name="y%d" % t)
+            for h in range(2):
+                banks[t, h] = full[t][:, h * HALF : (h + 1) * HALF]
+        for h in range(2):
+            xw = alloc("xw%d" % h, [P, HALF], U32)
+            nc.vector.tensor_copy(xw[:], xw_win[:].bitcast(U32).indirect(offs_sb[:, h * 16 : (h + 1) * 16]))
+            for t in range(PACK):
+                nc.tensor.matmul_mx(
+                    out=banks[t, h],
+                    lhsT=w1_codes[:, t * P : (t + 1) * P].bitcast(FP8X4),
+                    lhsT_scale=w1_scales[:, t * P : (t + 1) * P],
+                    rhs=xw[:].bitcast(FP8X4),
+                    rhs_scale=xs[:, h * HALF : (h + 1) * HALF],
+                    start=True,
+                    stop=True,
+                )
+
+        sig = [alloc("sig%d" % t, [P, S], F32) for t in range(PACK)]
+        pre = [alloc("pre%d" % t, [P, S], F32) for t in range(PACK)]
+        gy = alloc("gy", [P, PACK, S], F32)
+
+        def pieces(t):
+            if t == 0:
+                return [(banks[0, h], slice(h * HALF, (h + 1) * HALF)) for h in range(2)]
+            return [(full[t][:], slice(0, S))]
+
+        def make_sig(t):
+            for src, cols in pieces(t):
+                nc.scalar.activation(sig[t][:, cols], src, ACT.Sigmoid, scale=2.0)
+
+        def make_pre(t):
+            for src, cols in pieces(t):
+                nc.scalar.activation(pre[t][:, cols], src, ACT.Copy, scale=2.0)
+
+        def make_gy(t):
+            nc.vector.tensor_scalar(gy[:, t, :], sig[t][:], -0.5, gain2[:, t : t + 1], ALU.add, ALU.mult)
+
+        n1, n12, n123, arg, th = {}, {}, {}, {}, {}
+        for c, (j0, n) in enumerate(CHUNKS):
+            n1[c] = alloc("n1_%d" % c, [P, PACK, n], F32)
+            n12[c] = alloc("n12_%d" % c, [P, PACK, n], F32)
+            n123[c] = alloc("n123_%d" % c, [P, PACK, n], F32)
+            arg[c] = alloc("arg_%d" % c, [P, PACK, n], F32)
+            th[c] = alloc("th_%d" % c, [P, PACK, n], F32)
+
+        def entries(r, c):
+            j0, n = CHUNKS[c]
+            return lists[r][:, j0 // 16 : (j0 + n) // 16]
+
+        def first_scalar(c, t):
+            nc.scalar.activation(n1[c][:, t, :], pre[t][:].indirect(entries(0, c)), ACT.Sigmoid)
+
+        def first_vector(c, t):
+            nc.vector.tensor_copy(n1[c][:, t, :], sig[t][:].indirect(entries(0, c)))
+
+        def second(c, t):
+            nc.vector.tensor_tensor(n12[c][:, t, :], sig[t][:].indirect(entries(1, c)), n1[c][:, t, :], ALU.add)
+
+        def third(c, t):
+            nc.vector.tensor_tensor(n123[c][:, t, :], sig[t][:].indirect(entries(2, c)), n12[c][:, t, :], ALU.add)
+
+        def argument(c, t0, t1):
+            j0, n = CHUNKS[c]
+            nc.vector.scalar_tensor_tensor(arg[c][:, t0:t1, :], n123[c][:, t0:t1, :], -1.5, gy[:, t0:t1, j0 : j0 + n], ALU.add, ALU.mult)
+
+        def turn(c, t):
+            nc.scalar.activation(th[c][:, t, :], arg[c][:, t, :], ACT.Tanh, scale=unscale[:, t : t + 1])
+
+        z_bf, z_codes, z_scales = {}, {}, {}
+
+        def make_z(c):
+            j0, n = CHUNKS[c]
+            z_bf[c] = alloc("z_bf%d" % c, [P, n, PACK], BF16)
+            nc.vector.tensor_tensor(
+                z_bf[c][:].rearrange("p (g i) t -> p g t i", i=RUN),
+                th[c][:].rearrange("p t (g i) -> p g t i", i=RUN),
+                gy[:, :, j0 : j0 + n].rearrange("p t (g i) -> p g t i", i=RUN),
+                ALU.mult,
+            )
+
+        def quant_z(c):
+            j0, n = CHUNKS[c]
+            z_codes[c] = alloc("z_codes%d" % c, [P, n], U32)
+            z_scales[c] = alloc("z_scales%d" % c, [P, n], U8)
+            nc.vector.quantize_mx(z_codes[c][:].bitcast(FP8X4), z_scales[c][:], z_bf[c][:].rearrange("p n t -> p (n t)"))
+
+        w2_bf = alloc("w2_bf", [P, N, PACK], BF16)
+        w2_codes = alloc("w2_codes", [P, N], U32)
+        w2_scales = alloc("w2_scales", [P, N], U8)
+
+        def cast_w2(engine_copy, c0, c1):
+            engine_copy(
+                w2_bf[:, c0:c1, :].rearrange("p (g i) t -> p g t i", i=RUN),
+                w2_raw[:, :, c0:c1].rearrange("p t (g i) -> p g t i", i=RUN),
+            )
+
+        def quant_w2():
+            nc.vector.quantize_mx(w2_codes[:].bitcast(FP8X4), w2_scales[:], w2_bf[:].rearrange("p n t -> p (n t)"))
+
+        out_rows = out.rearrange("(m p) j -> p m j", p=P)
+
+        def product2(c, tags, copies, queues):
+            j0, n = CHUNKS[c]
+            per = PACK // len(tags)
+            for b, tag in enumerate(tags):
+                bank = ps.tile([P, per, n], F32, name="o%d_%d" % (c, b), tag=tag)
+                for m in range(per):
+                    cols = slice((b * per + m) * P, (b * per + m + 1) * P)
+                    nc.tensor.matmul_mx(
+                        out=bank[:, m, :],
+                        lhsT=w2_codes[:, cols].bitcast(FP8X4),
+                        lhsT_scale=w2_scales[:, cols],
+                        rhs=z_codes[c][:].bitcast(FP8X4),
+                        rhs_scale=z_scales[c][:],
+                        start=True,
+                        stop=True,
+                    )
+                res = alloc("res%d_%d" % (c, b), [P, per, n], F32)
+                copies[b](res[:], bank[:])
+                queues[b].dma_start(out_rows[:, b * per : (b + 1) * per, j0 : j0 + n], res[:])
+
+        make_sig(0)
+        first_vector(0, 0)
+        make_gy(0)
+        make_sig(1)
+        make_pre(1)
+        first_scalar(0, 1)
+        second(0, 0)
+        make_gy(1)
+        third(0, 0)
+        make_sig(2)
+        make_pre(2)
+        first_scalar(0, 2)
+        second(0, 1)
+        argument(0, 0, 1)
+        third(0, 1)
+        make_sig(3)
+        turn(0, 0)
+        make_pre(3)
+        first_scalar(0, 3)
+        make_gy(2)
+        second(0, 2)
+        argument(0, 1, 2)
+        third(0, 2)
+        turn(0, 1)
+        make_pre(0)
+        make_gy(3)
+        second(0, 3)
+        argument(0, 2, 3)
+        third(0, 3)
+        turn(0, 2)
+        for t in range(PACK):
+            first_scalar(1, t)
+        cast_w2(nc.vector.tensor_copy, 0, 256)
+        argument(0, 3, 4)
+        turn(0, 3)
+        cast_w2(nc.scalar.copy, 256, 512)
+        second(1, 0)
+        second(1, 1)
+        third(1, 0)
+        third(1, 1)
+        make_z(0)
+        for t in range(PACK):
+            first_scalar(2, t)
+        second(1, 2)
+        argument(1, 0, 2)
+        quant_z(0)
+        turn(1, 0)
+        turn(1, 1)
+        second(1, 3)
+        third(1, 2)
+        third(1, 3)
+        quant_w2()
+        argument(1, 2, 4)
+        turn(1, 2)
+        turn(1, 3)
+        product2(0, ("bankC", "bankD"), (nc.scalar.copy, nc.scalar.copy), (nc.sync, nc.sync))
+        second(2, 0)
+        second(2, 1)
+        third(2, 0)
+        third(2, 1)
+        make_z(1)
+        second(2, 2)
+        argument(2, 0, 2)
+        quant_z(1)
+        turn(2, 0)
+        turn(2, 1)
+        second(2, 3)
+        third(2, 2)
+        third(2, 3)
+        argument(2, 2, 3)
+        argument(2, 3, 4)
+        turn(2, 2)
+        turn(2, 3)
+        product2(1, ("bankE",), (nc.scalar.copy,), (nc.sync,))
+        make_z(2)
+        quant_z(2)
+        product2(2, ("bankA", "bankB"), (nc.vector.tensor_copy, nc.scalar.copy), (nc.sync, nc.scalar))

@@ -38,24 +38,29 @@ def tile_picked_isingm_none_p_kernel(tc, x_words, x_scales, w1, gn, w2, offs, p1
         xs_win = alloc("xs_win", [P, T], U8)
         xw_win = alloc("xw_win", [P, T], I32)
         w1_raw = alloc("w1_raw", [P, PACK, H], F32)
-        w2_raw = alloc("w2_raw", [P, PACK, N], F32)
         gn_sb = alloc("gn_sb", [P, PACK], F32)
         warm = alloc("warm", [P, 1], F32)
         warm_out = alloc("warm_out", [P, 1], F32)
 
-        nc.vector.memset(xs_win[:].bitcast(I32), 0)
-        nc.gpsimd.memset(warm[:], 0.0)
-        nc.scalar.activation(warm_out[:], warm[:], ACT.Sigmoid)
-
+        xs_rows = alloc("xs_rows", [P, T // 4], I32)
+        for q in range(4):
+            (nc.scalar, nc.sync)[q % 2].dma_start(xs_rows[32 * q : 32 * q + 4, :], x_scales[0, 4 * q : 4 * q + 4, :].bitcast(I32))
         nc.sync.dma_start(offs_sb[:], offs)
         nc.sync.dma_start(w1_raw[:], w1.rearrange("(p j) c -> p j c", j=PACK))
-        for q in range(4):
-            nc.sync.dma_start(xs_win[32 * q : 32 * q + 4, :].bitcast(I32), x_scales[0, 4 * q : 4 * q + 4, :].bitcast(I32))
-        nc.sync.dma_start(gn_sb[:], gn.rearrange("(p t) o -> p (t o)", t=PACK))
         nc.sync.dma_start(xw_win[:], x_words[0].rearrange("p n t -> p (n t)").bitcast(I32))
+        nc.sync.dma_start(gn_sb[:], gn.rearrange("(p t) o -> p (t o)", t=PACK))
         for lst, src in zip(lists, (p1, p2, p3)):
             nc.sync.dma_start(lst[:], src)
+        w2_raw = alloc("w2_raw", [P, PACK, N], F32)
         nc.sync.dma_start(w2_raw[:], w2.rearrange("(p j) c -> p j c", j=PACK))
+
+        nc.gpsimd.memset(warm[:], 0.0)
+        nc.scalar.activation(warm_out[:], warm[:], ACT.Sigmoid)
+        nc.vector.memset(xs_win[:].bitcast(I32), 0)
+        for q in range(4):
+            nc.vector.tensor_copy(xs_win[32 * q : 32 * q + 4, :].bitcast(I32), xs_rows[32 * q : 32 * q + 4, :])
+        xs = alloc("xs", [P, S], U8)
+        nc.vector.tensor_copy(xs[:], xs_win[:].indirect(offs_sb[:]))
 
         w1_bf = alloc("w1_bf", [P, PACK, P, PACK], BF16)
         w1_src = w1_raw[:].rearrange("p j (m t) -> p m j t", t=PACK)
@@ -67,17 +72,10 @@ def tile_picked_isingm_none_p_kernel(tc, x_words, x_scales, w1, gn, w2, offs, p1
         recip = alloc("recip", [P, PACK], F32)
         recip_hi = alloc("recip_hi", [P, PACK], F32)
         unscale = alloc("unscale", [P, PACK], F32)
-        nc.vector.tensor_scalar(gain2[:], gn_sb[:], 2.0, None, ALU.mult)
-        nc.vector.reciprocal(recip[:], gn_sb[:])
 
         w1_codes = alloc("w1_codes", [P, H], U32)
         w1_scales = alloc("w1_scales", [P, H], U8)
         nc.vector.quantize_mx(w1_codes[:].bitcast(FP8X4), w1_scales[:], w1_bf[:].rearrange("p t m j -> p (t m j)"))
-        nc.vector.tensor_scalar(recip_hi[:], recip[:], 2.0, BIG, ALU.mult, ALU.min)
-
-        xs = alloc("xs", [P, S], U8)
-        nc.vector.tensor_copy(xs[:], xs_win[:].indirect(offs_sb[:]))
-        nc.vector.tensor_scalar(unscale[:], recip_hi[:], -BIG, None, ALU.max)
 
         banks = {}
         banks[0, 0] = ps.tile([P, HALF], F32, name="y00", tag="bankA")[:]
@@ -87,19 +85,26 @@ def tile_picked_isingm_none_p_kernel(tc, x_words, x_scales, w1, gn, w2, offs, p1
             full[t] = ps.tile([P, S], F32, name="y%d" % t)
             for h in range(2):
                 banks[t, h] = full[t][:, h * HALF : (h + 1) * HALF]
+        xw = [alloc("xw%d" % h, [P, HALF], U32) for h in range(2)]
         for h in range(2):
-            xw = alloc("xw%d" % h, [P, HALF], U32)
-            nc.vector.tensor_copy(xw[:], xw_win[:].bitcast(U32).indirect(offs_sb[:, h * 16 : (h + 1) * 16]))
-            for t in range(PACK):
-                nc.tensor.matmul_mx(
-                    out=banks[t, h],
-                    lhsT=w1_codes[:, t * P : (t + 1) * P].bitcast(FP8X4),
-                    lhsT_scale=w1_scales[:, t * P : (t + 1) * P],
-                    rhs=xw[:].bitcast(FP8X4),
-                    rhs_scale=xs[:, h * HALF : (h + 1) * HALF],
-                    start=True,
-                    stop=True,
-                )
+            nc.vector.tensor_copy(xw[h][:], xw_win[:].bitcast(U32).indirect(offs_sb[:, h * 16 : (h + 1) * 16]))
+        for t0 in range(0, PACK, 2):
+            for h in range(2):
+                for t in (t0, t0 + 1):
+                    nc.tensor.matmul_mx(
+                        out=banks[t, h],
+                        lhsT=w1_codes[:, t * P : (t + 1) * P].bitcast(FP8X4),
+                        lhsT_scale=w1_scales[:, t * P : (t + 1) * P],
+                        rhs=xw[h][:].bitcast(FP8X4),
+                        rhs_scale=xs[:, h * HALF : (h + 1) * HALF],
+                        start=True,
+                        stop=True,
+                    )
+
+        nc.vector.reciprocal(recip[:], gn_sb[:])
+        nc.vector.tensor_scalar(gain2[:], gn_sb[:], 2.0, None, ALU.mult)
+        nc.vector.tensor_scalar(recip_hi[:], recip[:], 2.0, BIG, ALU.mult, ALU.min)
+        nc.vector.tensor_scalar(unscale[:], recip_hi[:], -BIG, None, ALU.max)
 
         sig = [alloc("sig%d" % t, [P, S], F32) for t in range(PACK)]
         pre = [alloc("pre%d" % t, [P, S], F32) for t in range(PACK)]
@@ -121,9 +126,11 @@ def tile_picked_isingm_none_p_kernel(tc, x_words, x_scales, w1, gn, w2, offs, p1
         def make_gy(t):
             nc.vector.tensor_scalar(gy[:, t, :], sig[t][:], -0.5, gain2[:, t : t + 1], ALU.add, ALU.mult)
 
-        n1, n12, n123, arg, th = {}, {}, {}, {}, {}
+        n1, n2, n12, n123, arg, th = {}, {}, {}, {}, {}, {}
         for c, (j0, n) in enumerate(CHUNKS):
             n1[c] = alloc("n1_%d" % c, [P, PACK, n], F32)
+            if c > 0:
+                n2[c] = alloc("n2_%d" % c, [P, PACK, n], F32)
             n12[c] = alloc("n12_%d" % c, [P, PACK, n], F32)
             n123[c] = alloc("n123_%d" % c, [P, PACK, n], F32)
             arg[c] = alloc("arg_%d" % c, [P, PACK, n], F32)
@@ -148,6 +155,19 @@ def tile_picked_isingm_none_p_kernel(tc, x_words, x_scales, w1, gn, w2, offs, p1
         def argument(c, t0, t1):
             j0, n = CHUNKS[c]
             nc.vector.scalar_tensor_tensor(arg[c][:, t0:t1, :], n123[c][:, t0:t1, :], -1.5, gy[:, t0:t1, j0 : j0 + n], ALU.add, ALU.mult)
+
+        def second_scalar(c, t):
+            nc.scalar.activation(n2[c][:, t, :], pre[t][:].indirect(entries(1, c)), ACT.Sigmoid)
+
+        def third_on_first(c, t):
+            nc.vector.tensor_tensor(n12[c][:, t, :], sig[t][:].indirect(entries(2, c)), n1[c][:, t, :], ALU.add)
+
+        def field(c, t0, t1):
+            nc.vector.scalar_tensor_tensor(n123[c][:, t0:t1, :], n12[c][:, t0:t1, :], -1.5, n2[c][:, t0:t1, :], ALU.add, ALU.add)
+
+        def times(c, t0, t1):
+            j0, n = CHUNKS[c]
+            nc.vector.tensor_tensor(arg[c][:, t0:t1, :], n123[c][:, t0:t1, :], gy[:, t0:t1, j0 : j0 + n], ALU.mult)
 
         def turn(c, t):
             nc.scalar.activation(th[c][:, t, :], arg[c][:, t, :], ACT.Tanh, scale=unscale[:, t : t + 1])
@@ -205,79 +225,71 @@ def tile_picked_isingm_none_p_kernel(tc, x_words, x_scales, w1, gn, w2, offs, p1
                 copies[b](res[:], bank[:])
                 queues[b].dma_start(out_rows[:, b * per : (b + 1) * per, j0 : j0 + n], res[:])
 
+        def both_scalar(c, t0):
+            for t in (t0, t0 + 1):
+                first_scalar(c, t)
+                second_scalar(c, t)
+
         make_sig(0)
         first_vector(0, 0)
         make_gy(0)
-        make_sig(1)
-        make_pre(1)
-        first_scalar(0, 1)
-        second(0, 0)
-        make_gy(1)
-        third(0, 0)
-        make_sig(2)
-        make_pre(2)
-        first_scalar(0, 2)
-        second(0, 1)
-        argument(0, 0, 1)
-        third(0, 1)
-        make_sig(3)
-        turn(0, 0)
-        make_pre(3)
-        first_scalar(0, 3)
-        make_gy(2)
-        second(0, 2)
-        argument(0, 1, 2)
-        third(0, 2)
-        turn(0, 1)
-        make_pre(0)
-        make_gy(3)
-        second(0, 3)
-        argument(0, 2, 3)
-        third(0, 3)
-        turn(0, 2)
         for t in range(PACK):
-            first_scalar(1, t)
-        cast_w2(nc.vector.tensor_copy, 0, 256)
+            if t + 1 < PACK:
+                make_sig(t + 1)
+                make_pre(t + 1)
+                first_scalar(0, t + 1)
+            else:
+                make_pre(0)
+                both_scalar(1, 0)
+            second(0, t)
+            if t > 0:
+                argument(0, t - 1, t)
+                turn(0, t - 1)
+            else:
+                make_gy(1)
+            third(0, t)
+            if 0 < t < PACK - 1:
+                make_gy(t + 1)
+        both_scalar(1, 2)
+        third_on_first(1, 0)
+        third_on_first(1, 1)
         argument(0, 3, 4)
         turn(0, 3)
-        cast_w2(nc.scalar.copy, 256, 512)
-        second(1, 0)
-        second(1, 1)
-        third(1, 0)
-        third(1, 1)
-        make_z(0)
-        for t in range(PACK):
-            first_scalar(2, t)
-        second(1, 2)
-        argument(1, 0, 2)
-        quant_z(0)
+        field(1, 0, 2)
+        cast_w2(nc.scalar.copy, 0, 256)
+
+        both_scalar(2, 0)
+        third_on_first(1, 2)
+        third_on_first(1, 3)
+        times(1, 0, 2)
         turn(1, 0)
         turn(1, 1)
-        second(1, 3)
-        third(1, 2)
-        third(1, 3)
-        quant_w2()
-        argument(1, 2, 4)
+        field(1, 2, 4)
+        make_z(0)
+        cast_w2(nc.scalar.copy, 256, 512)
+
+        both_scalar(2, 2)
+        third_on_first(2, 0)
+        third_on_first(2, 1)
+        quant_z(0)
+        times(1, 2, 4)
         turn(1, 2)
         turn(1, 3)
+        field(2, 0, 2)
+        quant_w2()
         product2(0, ("bankC", "bankD"), (nc.scalar.copy, nc.scalar.copy), (nc.sync, nc.sync))
-        second(2, 0)
-        second(2, 1)
-        third(2, 0)
-        third(2, 1)
-        make_z(1)
-        second(2, 2)
-        argument(2, 0, 2)
-        quant_z(1)
+
+        third_on_first(2, 2)
+        third_on_first(2, 3)
+        times(2, 0, 2)
         turn(2, 0)
         turn(2, 1)
-        second(2, 3)
-        third(2, 2)
-        third(2, 3)
-        argument(2, 2, 3)
-        argument(2, 3, 4)
+        field(2, 2, 4)
+        make_z(1)
+        times(2, 2, 4)
         turn(2, 2)
         turn(2, 3)
+        quant_z(1)
         product2(1, ("bankE",), (nc.scalar.copy,), (nc.sync,))
         make_z(2)
         quant_z(2)

@@ -19,9 +19,9 @@ P = 128
 PACK = 4
 HALF = S // 2
 CHUNKS = ((0, 256), (256, 128), (384, 128))
-W1_VECTOR_COLS = 80
+W1_VECTOR_COLS = 64
 BIG = 3.0e38
-RUN = 4
+RUN = 2
 
 
 def tile_picked_isingm_none_p_kernel(tc, x_words, x_scales, w1, gn, w2, offs, p1, p2, p3, out):
@@ -45,14 +45,15 @@ def tile_picked_isingm_none_p_kernel(tc, x_words, x_scales, w1, gn, w2, offs, p1
         xs_rows = alloc("xs_rows", [P, T // 4], I32)
         for q in range(4):
             (nc.scalar, nc.sync)[q % 2].dma_start(xs_rows[32 * q : 32 * q + 4, :], x_scales[0, 4 * q : 4 * q + 4, :].bitcast(I32))
+        nc.scalar.dma_start(gn_sb[:], gn.rearrange("(p t) o -> p (t o)", t=PACK))
         nc.sync.dma_start(offs_sb[:], offs)
         nc.sync.dma_start(w1_raw[:], w1.rearrange("(p j) c -> p j c", j=PACK))
         nc.sync.dma_start(xw_win[:], x_words[0].rearrange("p n t -> p (n t)").bitcast(I32))
-        nc.sync.dma_start(gn_sb[:], gn.rearrange("(p t) o -> p (t o)", t=PACK))
         for lst, src in zip(lists, (p1, p2, p3)):
             nc.sync.dma_start(lst[:], src)
-        w2_raw = alloc("w2_raw", [P, PACK, N], F32)
-        nc.sync.dma_start(w2_raw[:], w2.rearrange("(p j) c -> p j c", j=PACK))
+        w2_raw = [alloc("w2_raw%d" % h, [P, PACK, N // 2], F32) for h in range(2)]
+        for h in range(2):
+            nc.sync.dma_start(w2_raw[h][:], w2.rearrange("(p j) c -> p j c", j=PACK)[:, :, h * (N // 2) : (h + 1) * (N // 2)])
 
         nc.gpsimd.memset(warm[:], 0.0)
         nc.scalar.activation(warm_out[:], warm[:], ACT.Sigmoid)
@@ -75,7 +76,17 @@ def tile_picked_isingm_none_p_kernel(tc, x_words, x_scales, w1, gn, w2, offs, p1
 
         w1_codes = alloc("w1_codes", [P, H], U32)
         w1_scales = alloc("w1_scales", [P, H], U8)
-        nc.vector.quantize_mx(w1_codes[:].bitcast(FP8X4), w1_scales[:], w1_bf[:].rearrange("p t m j -> p (t m j)"))
+
+        def quant_w1(t0):
+            cols = slice(t0 * P, (t0 + 2) * P)
+            nc.vector.quantize_mx(w1_codes[:, cols].bitcast(FP8X4), w1_scales[:, cols], w1_bf[:, t0 : t0 + 2].rearrange("p t m j -> p (t m j)"))
+
+        nc.vector.reciprocal(recip[:], gn_sb[:])
+        nc.vector.tensor_scalar(gain2[:], gn_sb[:], 2.0, None, ALU.mult)
+        nc.vector.tensor_scalar(recip_hi[:], recip[:], 2.0, BIG, ALU.mult, ALU.min)
+        nc.vector.tensor_scalar(unscale[:], recip_hi[:], -BIG, None, ALU.max)
+
+        quant_w1(0)
 
         banks = {}
         banks[0, 0] = ps.tile([P, HALF], F32, name="y00", tag="bankA")[:]
@@ -88,6 +99,7 @@ def tile_picked_isingm_none_p_kernel(tc, x_words, x_scales, w1, gn, w2, offs, p1
         xw = [alloc("xw%d" % h, [P, HALF], U32) for h in range(2)]
         for h in range(2):
             nc.vector.tensor_copy(xw[h][:], xw_win[:].bitcast(U32).indirect(offs_sb[:, h * 16 : (h + 1) * 16]))
+        quant_w1(2)
         for t0 in range(0, PACK, 2):
             for h in range(2):
                 for t in (t0, t0 + 1):
@@ -100,11 +112,6 @@ def tile_picked_isingm_none_p_kernel(tc, x_words, x_scales, w1, gn, w2, offs, p1
                         start=True,
                         stop=True,
                     )
-
-        nc.vector.reciprocal(recip[:], gn_sb[:])
-        nc.vector.tensor_scalar(gain2[:], gn_sb[:], 2.0, None, ALU.mult)
-        nc.vector.tensor_scalar(recip_hi[:], recip[:], 2.0, BIG, ALU.mult, ALU.min)
-        nc.vector.tensor_scalar(unscale[:], recip_hi[:], -BIG, None, ALU.max)
 
         sig = [alloc("sig%d" % t, [P, S], F32) for t in range(PACK)]
         pre = [alloc("pre%d" % t, [P, S], F32) for t in range(PACK)]
@@ -194,14 +201,15 @@ def tile_picked_isingm_none_p_kernel(tc, x_words, x_scales, w1, gn, w2, offs, p1
         w2_codes = alloc("w2_codes", [P, N], U32)
         w2_scales = alloc("w2_scales", [P, N], U8)
 
-        def cast_w2(engine_copy, c0, c1):
-            engine_copy(
-                w2_bf[:, c0:c1, :].rearrange("p (g i) t -> p g t i", i=RUN),
-                w2_raw[:, :, c0:c1].rearrange("p t (g i) -> p g t i", i=RUN),
+        def cast_w2(copy, h):
+            copy(
+                w2_bf[:, h * (N // 2) : (h + 1) * (N // 2), :].rearrange("p (g i) t -> p g t i", i=RUN),
+                w2_raw[h][:].rearrange("p t (g i) -> p g t i", i=RUN),
             )
 
-        def quant_w2():
-            nc.vector.quantize_mx(w2_codes[:].bitcast(FP8X4), w2_scales[:], w2_bf[:].rearrange("p n t -> p (n t)"))
+        def quant_w2(h):
+            cols = slice(h * (N // 2), (h + 1) * (N // 2))
+            nc.vector.quantize_mx(w2_codes[:, cols].bitcast(FP8X4), w2_scales[:, cols], w2_bf[:, cols, :].rearrange("p n t -> p (n t)"))
 
         out_rows = out.rearrange("(m p) j -> p m j", p=P)
 
@@ -231,7 +239,9 @@ def tile_picked_isingm_none_p_kernel(tc, x_words, x_scales, w1, gn, w2, offs, p1
                 second_scalar(c, t)
 
         make_sig(0)
+        cast_w2(nc.vector.tensor_copy, 0)
         first_vector(0, 0)
+        quant_w2(0)
         make_gy(0)
         for t in range(PACK):
             if t + 1 < PACK:
@@ -256,7 +266,7 @@ def tile_picked_isingm_none_p_kernel(tc, x_words, x_scales, w1, gn, w2, offs, p1
         argument(0, 3, 4)
         turn(0, 3)
         field(1, 0, 2)
-        cast_w2(nc.scalar.copy, 0, 256)
+        cast_w2(nc.scalar.copy, 1)
 
         both_scalar(2, 0)
         third_on_first(1, 2)
@@ -266,7 +276,6 @@ def tile_picked_isingm_none_p_kernel(tc, x_words, x_scales, w1, gn, w2, offs, p1
         turn(1, 1)
         field(1, 2, 4)
         make_z(0)
-        cast_w2(nc.scalar.copy, 256, 512)
 
         both_scalar(2, 2)
         third_on_first(2, 0)
@@ -276,7 +285,7 @@ def tile_picked_isingm_none_p_kernel(tc, x_words, x_scales, w1, gn, w2, offs, p1
         turn(1, 2)
         turn(1, 3)
         field(2, 0, 2)
-        quant_w2()
+        quant_w2(1)
         product2(0, ("bankC", "bankD"), (nc.scalar.copy, nc.scalar.copy), (nc.sync, nc.sync))
 
         third_on_first(2, 2)

@@ -1,6 +1,7 @@
 from contextlib import ExitStack
 
 import concourse.mybir as mybir
+from concourse.masks import make_identity
 
 K, T, S, N, H = 512, 2048, 512, 512, 512
 FLOPS = 2 * K * H * S + 2 * H * N * S
@@ -20,7 +21,9 @@ PACK = 4
 HALF = S // 2
 CHUNKS = ((0, 256), (256, 128), (384, 128))
 W1_VECTOR_COLS = 64
-BIG = 3.0e38
+VEC_TILES = (0, 2)
+SCA_TILES = (1, 3)
+TURN_BANKS = {(0, 1): ("bank0", "bank1"), (1, 1): ("bank2", "bank3"), (2, 1): ("bank6", "bank7"), (2, 3): ("bank0", "bank1")}
 RUN = 2
 
 
@@ -57,6 +60,8 @@ def tile_picked_isingm_none_p_kernel(tc, x_words, x_scales, w1, gn, w2, offs, p1
 
         nc.gpsimd.memset(warm[:], 0.0)
         nc.scalar.activation(warm_out[:], warm[:], ACT.Sigmoid)
+        ident = alloc("ident", [P, P], F32)
+        make_identity(nc, ident[:])
         nc.vector.memset(xs_win[:].bitcast(I32), 0)
         for q in range(4):
             nc.vector.tensor_copy(xs_win[32 * q : 32 * q + 4, :].bitcast(I32), xs_rows[32 * q : 32 * q + 4, :])
@@ -69,11 +74,6 @@ def tile_picked_isingm_none_p_kernel(tc, x_words, x_scales, w1, gn, w2, offs, p1
         nc.vector.tensor_copy(w1_dst[:, :W1_VECTOR_COLS], w1_src[:, :W1_VECTOR_COLS])
         nc.scalar.copy(w1_dst[:, W1_VECTOR_COLS:], w1_src[:, W1_VECTOR_COLS:])
 
-        gain2 = alloc("gain2", [P, PACK], F32)
-        recip = alloc("recip", [P, PACK], F32)
-        recip_hi = alloc("recip_hi", [P, PACK], F32)
-        unscale = alloc("unscale", [P, PACK], F32)
-
         w1_codes = alloc("w1_codes", [P, H], U32)
         w1_scales = alloc("w1_scales", [P, H], U8)
 
@@ -81,21 +81,15 @@ def tile_picked_isingm_none_p_kernel(tc, x_words, x_scales, w1, gn, w2, offs, p1
             cols = slice(t0 * P, (t0 + 2) * P)
             nc.vector.quantize_mx(w1_codes[:, cols].bitcast(FP8X4), w1_scales[:, cols], w1_bf[:, t0 : t0 + 2].rearrange("p t m j -> p (t m j)"))
 
-        nc.vector.reciprocal(recip[:], gn_sb[:])
-        nc.vector.tensor_scalar(gain2[:], gn_sb[:], 2.0, None, ALU.mult)
-        nc.vector.tensor_scalar(recip_hi[:], recip[:], 2.0, BIG, ALU.mult, ALU.min)
-        nc.vector.tensor_scalar(unscale[:], recip_hi[:], -BIG, None, ALU.max)
-
         quant_w1(0)
 
         banks = {}
-        banks[0, 0] = ps.tile([P, HALF], F32, name="y00", tag="bankA")[:]
-        banks[0, 1] = ps.tile([P, HALF], F32, name="y01", tag="bankB")[:]
-        full = {}
-        for t in range(1, PACK):
-            full[t] = ps.tile([P, S], F32, name="y%d" % t)
+        for t in range(2):
             for h in range(2):
-                banks[t, h] = full[t][:, h * HALF : (h + 1) * HALF]
+                banks[t, h] = ps.tile([P, HALF], F32, name="a%d%d" % (t, h), tag="bank%d" % (2 * t + h))
+        full = {}
+        for t in range(2, PACK):
+            full[t] = ps.tile([P, S], F32, name="a%d" % t, tag="bank%d" % (t + 2))
         xw = [alloc("xw%d" % h, [P, HALF], U32) for h in range(2)]
         for h in range(2):
             nc.vector.tensor_copy(xw[h][:], xw_win[:].bitcast(U32).indirect(offs_sb[:, h * 16 : (h + 1) * 16]))
@@ -104,7 +98,7 @@ def tile_picked_isingm_none_p_kernel(tc, x_words, x_scales, w1, gn, w2, offs, p1
             for h in range(2):
                 for t in (t0, t0 + 1):
                     nc.tensor.matmul_mx(
-                        out=banks[t, h],
+                        out=banks[t, h][:] if t < 2 else full[t][:, h * HALF : (h + 1) * HALF],
                         lhsT=w1_codes[:, t * P : (t + 1) * P].bitcast(FP8X4),
                         lhsT_scale=w1_scales[:, t * P : (t + 1) * P],
                         rhs=xw[h][:].bitcast(FP8X4),
@@ -113,80 +107,134 @@ def tile_picked_isingm_none_p_kernel(tc, x_words, x_scales, w1, gn, w2, offs, p1
                         stop=True,
                     )
 
-        sig = [alloc("sig%d" % t, [P, S], F32) for t in range(PACK)]
-        pre = [alloc("pre%d" % t, [P, S], F32) for t in range(PACK)]
+        spin = {t: alloc("spin%d" % t, [P, S], F32) for t in VEC_TILES}
+        pre = {t: sb.tile([P, S], F32, name="pre%d" % t, tag="pre%d" % t, align_bytes=64) for t in SCA_TILES}
+        spin_s = alloc("spin_s", [P, 2, S], F32)
         gy = alloc("gy", [P, PACK, S], F32)
 
         def pieces(t):
-            if t == 0:
-                return [(banks[0, h], slice(h * HALF, (h + 1) * HALF)) for h in range(2)]
+            if t < 2:
+                return [(banks[t, h][:], slice(h * HALF, (h + 1) * HALF)) for h in range(2)]
             return [(full[t][:], slice(0, S))]
 
-        def make_sig(t):
+        def make_spin(t):
             for src, cols in pieces(t):
-                nc.scalar.activation(sig[t][:, cols], src, ACT.Sigmoid, scale=2.0)
+                nc.scalar.activation(spin[t][:, cols], src, ACT.Tanh)
 
-        def make_pre(t):
+        def pre_vector(t):
+            for src, cols in pieces(t):
+                nc.vector.tensor_scalar(pre[t][:, cols], src, 2.0, None, ALU.mult)
+
+        def pre_scalar(t):
             for src, cols in pieces(t):
                 nc.scalar.activation(pre[t][:, cols], src, ACT.Copy, scale=2.0)
 
+        def spin_from_pre(t):
+            nc.scalar.activation(spin_s[:, t // 2, :], pre[t][:], ACT.Tanh, scale=0.5)
+
         def make_gy(t):
-            nc.vector.tensor_scalar(gy[:, t, :], sig[t][:], -0.5, gain2[:, t : t + 1], ALU.add, ALU.mult)
+            src = spin[t][:] if t in VEC_TILES else spin_s[:, t // 2, :]
+            nc.vector.tensor_scalar(gy[:, t, :], src, gn_sb[:, t : t + 1], None, ALU.mult)
 
-        n1, n2, n12, n123, arg, th = {}, {}, {}, {}, {}, {}
-        for c, (j0, n) in enumerate(CHUNKS):
-            n1[c] = alloc("n1_%d" % c, [P, PACK, n], F32)
-            if c > 0:
-                n2[c] = alloc("n2_%d" % c, [P, PACK, n], F32)
-            n12[c] = alloc("n12_%d" % c, [P, PACK, n], F32)
-            n123[c] = alloc("n123_%d" % c, [P, PACK, n], F32)
-            arg[c] = alloc("arg_%d" % c, [P, PACK, n], F32)
-            th[c] = alloc("th_%d" % c, [P, PACK, n], F32)
-
-        def entries(r, c):
-            j0, n = CHUNKS[c]
+        def entries(r, j0, n):
             return lists[r][:, j0 // 16 : (j0 + n) // 16]
 
-        def first_scalar(c, t):
-            nc.scalar.activation(n1[c][:, t, :], pre[t][:].indirect(entries(0, c)), ACT.Sigmoid)
+        part = {}
+        for c, (j0, n) in enumerate(CHUNKS):
+            for r in range(3):
+                part[c, r] = alloc("part%d_%d" % (c, r), [P, 2, n], F32)
+        arg = [alloc("arg%d" % h, [P, PACK, HALF], F32) for h in range(2)]
+        th = [alloc("th%d" % h, [P, PACK, HALF], F32) for h in range(2)]
 
-        def first_vector(c, t):
-            nc.vector.tensor_copy(n1[c][:, t, :], sig[t][:].indirect(entries(0, c)))
-
-        def second(c, t):
-            nc.vector.tensor_tensor(n12[c][:, t, :], sig[t][:].indirect(entries(1, c)), n1[c][:, t, :], ALU.add)
-
-        def third(c, t):
-            nc.vector.tensor_tensor(n123[c][:, t, :], sig[t][:].indirect(entries(2, c)), n12[c][:, t, :], ALU.add)
-
-        def argument(c, t0, t1):
+        def fetch_vector(c, r, t):
             j0, n = CHUNKS[c]
-            nc.vector.scalar_tensor_tensor(arg[c][:, t0:t1, :], n123[c][:, t0:t1, :], -1.5, gy[:, t0:t1, j0 : j0 + n], ALU.add, ALU.mult)
+            window = spin[t][:].indirect(entries(r, j0, n))
+            if r == 0:
+                nc.vector.tensor_copy(part[c, 0][:, t // 2, :], window)
+            else:
+                nc.vector.tensor_tensor(part[c, r][:, t // 2, :], window, part[c, r - 1][:, t // 2, :], ALU.add)
 
-        def second_scalar(c, t):
-            nc.scalar.activation(n2[c][:, t, :], pre[t][:].indirect(entries(1, c)), ACT.Sigmoid)
-
-        def third_on_first(c, t):
-            nc.vector.tensor_tensor(n12[c][:, t, :], sig[t][:].indirect(entries(2, c)), n1[c][:, t, :], ALU.add)
-
-        def field(c, t0, t1):
-            nc.vector.scalar_tensor_tensor(n123[c][:, t0:t1, :], n12[c][:, t0:t1, :], -1.5, n2[c][:, t0:t1, :], ALU.add, ALU.add)
-
-        def times(c, t0, t1):
+        def arg_vector(c, t):
             j0, n = CHUNKS[c]
-            nc.vector.tensor_tensor(arg[c][:, t0:t1, :], n123[c][:, t0:t1, :], gy[:, t0:t1, j0 : j0 + n], ALU.mult)
+            h, i0 = divmod(j0, HALF)
+            nc.vector.tensor_tensor(arg[h][:, t, i0 : i0 + n], part[c, 2][:, t // 2, :], spin[t][:, j0 : j0 + n], ALU.mult)
 
-        def turn(c, t):
-            nc.scalar.activation(th[c][:, t, :], arg[c][:, t, :], ACT.Tanh, scale=unscale[:, t : t + 1])
+        def turn_vec_tiles(c):
+            j0, n = CHUNKS[c]
+            h, i0 = divmod(j0, HALF)
+            nc.scalar.activation(th[h][:, 0::2, i0 : i0 + n], arg[h][:, 0::2, i0 : i0 + n], ACT.Tanh)
+
+        sig = {}
+        for c, (j0, n) in enumerate(CHUNKS):
+            for t in SCA_TILES:
+                for r in range(3):
+                    sig[c, t, r] = alloc("sig%d_%d_%d" % (c, t, r), [P, n], F32)
+        turned, turned_sb, field = {}, {}, {}
+
+        def fetch_scalar(c, t, r):
+            j0, n = CHUNKS[c]
+            nc.scalar.activation(sig[c, t, r][:], pre[t][:].indirect(entries(r, j0, n)), ACT.Sigmoid)
+
+        def group_of(c, t):
+            return SCA_TILES if c < 2 else (t,)
+
+        def rows(tiles):
+            return slice(tiles[0], tiles[-1] + 1, 2)
+
+        def sum_turned(c, t):
+            blocks = CHUNKS[c][1] // P
+            tiles = group_of(c, t)
+            if t == tiles[0]:
+                turned[c, tiles] = ps.tile([P, len(tiles), blocks, P], F32, name="turned%d_%d" % (c, t), tag=TURN_BANKS[c, t][0])
+            for jb in range(blocks):
+                for r in range(3):
+                    nc.tensor.matmul(
+                        turned[c, tiles][:, tiles.index(t), jb, :], sig[c, t, r][:, jb * P : (jb + 1) * P], ident[:], start=(r == 0), stop=(r == 2), is_transpose=True
+                    )
+
+        def turn_back(c, tiles, on_vector):
+            blocks = CHUNKS[c][1] // P
+            staged = alloc("turned_sb%d_%d" % (c, tiles[0]), [P, len(tiles), blocks, P], F32)
+            if on_vector:
+                nc.vector.tensor_scalar(staged[:], turned[c, tiles][:], 2.0, None, ALU.mult)
+            else:
+                nc.scalar.activation(staged[:], turned[c, tiles][:], ACT.Copy, scale=2.0)
+            field[c, tiles] = ps.tile([P, len(tiles), blocks, P], F32, name="field%d_%d" % (c, tiles[0]), tag=TURN_BANKS[c, tiles[0]][1])
+            for b in range(len(tiles)):
+                for jb in range(blocks):
+                    nc.tensor.transpose(field[c, tiles][:, b, jb, :], staged[:, b, jb, :], ident[:])
+
+        def arg_sca_tiles(c, tiles):
+            j0, n = CHUNKS[c]
+            h, i0 = divmod(j0, HALF)
+            nc.vector.scalar_tensor_tensor(
+                arg[h][:, rows(tiles), i0 : i0 + n],
+                field[c, tiles][:].rearrange("p b k j -> p b (k j)"),
+                -3.0,
+                spin_s[:, tiles[0] // 2 : tiles[-1] // 2 + 1, j0 : j0 + n],
+                ALU.add,
+                ALU.mult,
+            )
+
+        def turn_sca_tiles(c, tiles):
+            j0, n = CHUNKS[c]
+            h, i0 = divmod(j0, HALF)
+            nc.scalar.activation(th[h][:, rows(tiles), i0 : i0 + n], arg[h][:, rows(tiles), i0 : i0 + n], ACT.Tanh)
+
+        def fetch_tile_scalar(c, t):
+            for r in range(3):
+                fetch_scalar(c, t, r)
+            sum_turned(c, t)
 
         z_bf, z_codes, z_scales = {}, {}, {}
 
         def make_z(c):
             j0, n = CHUNKS[c]
+            h, i0 = divmod(j0, HALF)
             z_bf[c] = alloc("z_bf%d" % c, [P, n, PACK], BF16)
             nc.vector.tensor_tensor(
                 z_bf[c][:].rearrange("p (g i) t -> p g t i", i=RUN),
-                th[c][:].rearrange("p t (g i) -> p g t i", i=RUN),
+                th[h][:, :, i0 : i0 + n].rearrange("p t (g i) -> p g t i", i=RUN),
                 gy[:, :, j0 : j0 + n].rearrange("p t (g i) -> p g t i", i=RUN),
                 ALU.mult,
             )
@@ -197,19 +245,21 @@ def tile_picked_isingm_none_p_kernel(tc, x_words, x_scales, w1, gn, w2, offs, p1
             z_scales[c] = alloc("z_scales%d" % c, [P, n], U8)
             nc.vector.quantize_mx(z_codes[c][:].bitcast(FP8X4), z_scales[c][:], z_bf[c][:].rearrange("p n t -> p (n t)"))
 
-        w2_bf = alloc("w2_bf", [P, N, PACK], BF16)
+        w2_bf = {}
         w2_codes = alloc("w2_codes", [P, N], U32)
         w2_scales = alloc("w2_scales", [P, N], U8)
 
-        def cast_w2(copy, h):
+        def cast_w2(copy, h, i0, n, tag):
+            if i0 == 0:
+                w2_bf[h] = sb.tile([P, N // 2, PACK], BF16, name="w2_bf%d" % h, tag=tag, align_bytes=64)
             copy(
-                w2_bf[:, h * (N // 2) : (h + 1) * (N // 2), :].rearrange("p (g i) t -> p g t i", i=RUN),
-                w2_raw[h][:].rearrange("p t (g i) -> p g t i", i=RUN),
+                w2_bf[h][:, i0 : i0 + n, :].rearrange("p (g i) t -> p g t i", i=RUN),
+                w2_raw[h][:, :, i0 : i0 + n].rearrange("p t (g i) -> p g t i", i=RUN),
             )
 
         def quant_w2(h):
             cols = slice(h * (N // 2), (h + 1) * (N // 2))
-            nc.vector.quantize_mx(w2_codes[:, cols].bitcast(FP8X4), w2_scales[:, cols], w2_bf[:, cols, :].rearrange("p n t -> p (n t)"))
+            nc.vector.quantize_mx(w2_codes[:, cols].bitcast(FP8X4), w2_scales[:, cols], w2_bf[h][:].rearrange("p n t -> p (n t)"))
 
         out_rows = out.rearrange("(m p) j -> p m j", p=P)
 
@@ -233,73 +283,70 @@ def tile_picked_isingm_none_p_kernel(tc, x_words, x_scales, w1, gn, w2, offs, p1
                 copies[b](res[:], bank[:])
                 queues[b].dma_start(out_rows[:, b * per : (b + 1) * per, j0 : j0 + n], res[:])
 
-        def both_scalar(c, t0):
-            for t in (t0, t0 + 1):
-                first_scalar(c, t)
-                second_scalar(c, t)
-
-        make_sig(0)
-        cast_w2(nc.vector.tensor_copy, 0)
-        first_vector(0, 0)
-        quant_w2(0)
+        make_spin(0)
+        pre_vector(1)
+        cast_w2(nc.vector.tensor_copy, 0, 0, P, "w2_bf0")
+        cast_w2(nc.scalar.copy, 0, P, P, "w2_bf0")
+        fetch_scalar(0, 1, 0)
+        make_spin(2)
+        fetch_scalar(0, 1, 1)
+        fetch_scalar(0, 1, 2)
+        sum_turned(0, 1)
+        fetch_vector(0, 0, 0)
+        pre_vector(3)
+        fetch_vector(0, 1, 0)
         make_gy(0)
-        for t in range(PACK):
-            if t + 1 < PACK:
-                make_sig(t + 1)
-                make_pre(t + 1)
-                first_scalar(0, t + 1)
-            else:
-                make_pre(0)
-                both_scalar(1, 0)
-            second(0, t)
-            if t > 0:
-                argument(0, t - 1, t)
-                turn(0, t - 1)
-            else:
-                make_gy(1)
-            third(0, t)
-            if 0 < t < PACK - 1:
-                make_gy(t + 1)
-        both_scalar(1, 2)
-        third_on_first(1, 0)
-        third_on_first(1, 1)
-        argument(0, 3, 4)
-        turn(0, 3)
-        field(1, 0, 2)
-        cast_w2(nc.scalar.copy, 1)
-
-        both_scalar(2, 0)
-        third_on_first(1, 2)
-        third_on_first(1, 3)
-        times(1, 0, 2)
-        turn(1, 0)
-        turn(1, 1)
-        field(1, 2, 4)
+        fetch_vector(0, 2, 0)
+        fetch_vector(0, 0, 2)
+        arg_vector(0, 0)
+        fetch_vector(0, 1, 2)
+        quant_w2(0)
+        fetch_vector(0, 2, 2)
+        make_gy(2)
+        arg_vector(0, 2)
+        fetch_tile_scalar(0, 3)
+        spin_from_pre(1)
+        spin_from_pre(3)
+        turn_back(0, SCA_TILES, False)
+        fetch_tile_scalar(1, 1)
+        turn_vec_tiles(0)
+        arg_sca_tiles(0, SCA_TILES)
+        fetch_tile_scalar(1, 3)
+        turn_sca_tiles(0, SCA_TILES)
+        for r in range(3):
+            for t in VEC_TILES:
+                fetch_vector(1, r, t)
+        make_gy(1)
+        make_gy(3)
+        turn_back(1, SCA_TILES, True)
+        fetch_tile_scalar(2, 1)
+        fetch_tile_scalar(2, 3)
         make_z(0)
-
-        both_scalar(2, 2)
-        third_on_first(2, 0)
-        third_on_first(2, 1)
+        arg_vector(1, 0)
+        arg_vector(1, 2)
         quant_z(0)
-        times(1, 2, 4)
-        turn(1, 2)
-        turn(1, 3)
-        field(2, 0, 2)
-        quant_w2(1)
-        product2(0, ("bankC", "bankD"), (nc.scalar.copy, nc.scalar.copy), (nc.sync, nc.sync))
-
-        third_on_first(2, 2)
-        third_on_first(2, 3)
-        times(2, 0, 2)
-        turn(2, 0)
-        turn(2, 1)
-        field(2, 2, 4)
+        arg_sca_tiles(1, SCA_TILES)
+        turn_back(2, (1,), False)
+        turn_vec_tiles(1)
+        turn_back(2, (3,), False)
+        turn_sca_tiles(1, SCA_TILES)
+        cast_w2(nc.scalar.copy, 1, 0, P, "pre1")
+        cast_w2(nc.scalar.copy, 1, P, P, "pre1")
+        for r in range(3):
+            for t in VEC_TILES:
+                fetch_vector(2, r, t)
+        arg_sca_tiles(2, (1,))
+        arg_vector(2, 0)
+        arg_vector(2, 2)
+        arg_sca_tiles(2, (3,))
+        turn_sca_tiles(2, (1,))
+        turn_vec_tiles(2)
+        turn_sca_tiles(2, (3,))
         make_z(1)
-        times(2, 2, 4)
-        turn(2, 2)
-        turn(2, 3)
+        quant_w2(1)
+        product2(0, ("bank4", "bank5"), (nc.scalar.copy, nc.scalar.copy), (nc.sync, nc.sync))
         quant_z(1)
-        product2(1, ("bankE",), (nc.scalar.copy,), (nc.sync,))
+        product2(1, ("bank2",), (nc.scalar.copy,), (nc.sync,))
         make_z(2)
         quant_z(2)
-        product2(2, ("bankA", "bankB"), (nc.vector.tensor_copy, nc.scalar.copy), (nc.sync, nc.scalar))
+        product2(2, ("bank3", "bank6"), (nc.vector.tensor_copy, nc.scalar.copy), (nc.sync, nc.scalar))

@@ -23,8 +23,9 @@ CHUNKS = ((0, 256), (256, 128), (384, 128))
 W1_VECTOR_COLS = 64
 VEC_TILES = (0, 2)
 SCA_TILES = (1, 3)
-TURN_BANKS = {(0, 1): ("bank0", "bank1"), (1, 1): ("bank2", "bank3"), (2, 1): ("bank6", "bank7"), (2, 3): ("bank0", "bank1")}
+TURN_BANKS = {(0, 1): ("bank0", "bank1"), (1, 1): ("bank2", "bank3"), (2, 1): ("bank6", "bank7"), (2, 3): ("bank2", "bank1")}
 RUN = 2
+RES_TAGS = {(0, 1): "arg"}
 
 
 def tile_picked_isingm_none_p_kernel(tc, x_words, x_scales, w1, gn, w2, offs, p1, p2, p3, out):
@@ -90,26 +91,31 @@ def tile_picked_isingm_none_p_kernel(tc, x_words, x_scales, w1, gn, w2, offs, p1
         full = {}
         for t in range(2, PACK):
             full[t] = ps.tile([P, S], F32, name="a%d" % t, tag="bank%d" % (t + 2))
-        xw = [alloc("xw%d" % h, [P, HALF], U32) for h in range(2)]
+        xw = alloc("xw", [P, S], U32)
         for h in range(2):
-            nc.vector.tensor_copy(xw[h][:], xw_win[:].bitcast(U32).indirect(offs_sb[:, h * 16 : (h + 1) * 16]))
+            nc.vector.tensor_copy(xw[:, h * HALF : (h + 1) * HALF], xw_win[:].bitcast(U32).indirect(offs_sb[:, h * 16 : (h + 1) * 16]))
         quant_w1(2)
-        for t0 in range(0, PACK, 2):
-            for h in range(2):
-                for t in (t0, t0 + 1):
-                    nc.tensor.matmul_mx(
-                        out=banks[t, h][:] if t < 2 else full[t][:, h * HALF : (h + 1) * HALF],
-                        lhsT=w1_codes[:, t * P : (t + 1) * P].bitcast(FP8X4),
-                        lhsT_scale=w1_scales[:, t * P : (t + 1) * P],
-                        rhs=xw[h][:].bitcast(FP8X4),
-                        rhs_scale=xs[:, h * HALF : (h + 1) * HALF],
-                        start=True,
-                        stop=True,
-                    )
+
+        def product1(dst, t, cols):
+            nc.tensor.matmul_mx(
+                out=dst,
+                lhsT=w1_codes[:, t * P : (t + 1) * P].bitcast(FP8X4),
+                lhsT_scale=w1_scales[:, t * P : (t + 1) * P],
+                rhs=xw[:, cols].bitcast(FP8X4),
+                rhs_scale=xs[:, cols],
+                start=True,
+                stop=True,
+            )
+
+        for h in range(2):
+            for t in range(2):
+                product1(banks[t, h][:], t, slice(h * HALF, (h + 1) * HALF))
+        for t in range(2, PACK):
+            product1(full[t][:], t, slice(0, S))
 
         spin = {t: alloc("spin%d" % t, [P, S], F32) for t in VEC_TILES}
         pre = {t: sb.tile([P, S], F32, name="pre%d" % t, tag="pre%d" % t, align_bytes=64) for t in SCA_TILES}
-        spin_s = alloc("spin_s", [P, 2, S], F32)
+        spin_turned = alloc("spin_turned", [P, 2, S // P, P], F32)
         gy = alloc("gy", [P, PACK, S], F32)
 
         def pieces(t):
@@ -121,120 +127,111 @@ def tile_picked_isingm_none_p_kernel(tc, x_words, x_scales, w1, gn, w2, offs, p1
             for src, cols in pieces(t):
                 nc.scalar.activation(spin[t][:, cols], src, ACT.Tanh)
 
-        def pre_vector(t):
+        def make_pre(t, on_vector):
             for src, cols in pieces(t):
-                nc.vector.tensor_scalar(pre[t][:, cols], src, 2.0, None, ALU.mult)
+                if on_vector:
+                    nc.vector.tensor_scalar(pre[t][:, cols], src, 2.0, None, ALU.mult)
+                else:
+                    nc.scalar.activation(pre[t][:, cols], src, ACT.Copy, scale=2.0)
 
-        def pre_scalar(t):
-            for src, cols in pieces(t):
-                nc.scalar.activation(pre[t][:, cols], src, ACT.Copy, scale=2.0)
+        pre_turned, spin_back = {}, {}
 
-        def spin_from_pre(t):
-            nc.scalar.activation(spin_s[:, t // 2, :], pre[t][:], ACT.Tanh, scale=0.5)
+        def turn_pre(t):
+            pre_turned[t] = ps.tile([P, S // P, P], F32, name="pre_turned%d" % t, tag="bank%d" % (6 + t // 2))
+            for jb in range(S // P):
+                nc.tensor.transpose(pre_turned[t][:, jb, :], pre[t][:, jb * P : (jb + 1) * P], ident[:])
 
-        def make_gy(t):
-            src = spin[t][:] if t in VEC_TILES else spin_s[:, t // 2, :]
-            nc.vector.tensor_scalar(gy[:, t, :], src, gn_sb[:, t : t + 1], None, ALU.mult)
+        def make_spin_turned(t):
+            nc.scalar.activation(spin_turned[:, t // 2], pre_turned[t][:], ACT.Tanh, scale=0.5)
+            spin_back[t] = ps.tile([P, S // P, P], F32, name="spin_back%d" % t, tag="bank%d" % (4 + t // 2))
+            for jb in range(S // P):
+                nc.tensor.transpose(spin_back[t][:, jb, :], spin_turned[:, t // 2, jb, :], ident[:])
+
+        def make_gy(t, on_vector):
+            src = spin[t][:] if t in VEC_TILES else spin_back[t][:].rearrange("p k j -> p (k j)")
+            if on_vector:
+                nc.vector.tensor_scalar(gy[:, t, :], src, gn_sb[:, t : t + 1], None, ALU.mult)
+            else:
+                nc.scalar.activation(gy[:, t, :], src, ACT.Copy, scale=gn_sb[:, t : t + 1])
 
         def entries(r, j0, n):
             return lists[r][:, j0 // 16 : (j0 + n) // 16]
 
-        part = {}
-        for c, (j0, n) in enumerate(CHUNKS):
-            for r in range(3):
-                part[c, r] = alloc("part%d_%d" % (c, r), [P, 2, n], F32)
-        arg = [alloc("arg%d" % h, [P, PACK, HALF], F32) for h in range(2)]
-        th = [alloc("th%d" % h, [P, PACK, HALF], F32) for h in range(2)]
+        first = alloc("first", [P, 2, S], F32)
+        third = alloc("third", [P, 2, S], F32)
+        second = {}
+        arg = sb.tile([P, 2, S], F32, name="arg", tag="arg", align_bytes=64)
+        th = alloc("th", [P, PACK, S], F32)
 
-        def fetch_vector(c, r, t):
+        def fetch_first(t, j0, n):
+            nc.vector.tensor_copy(first[:, t // 2, j0 : j0 + n], spin[t][:].indirect(entries(0, j0, n)))
+
+        def fetch_second(c, t, dst):
             j0, n = CHUNKS[c]
-            window = spin[t][:].indirect(entries(r, j0, n))
-            if r == 0:
-                nc.vector.tensor_copy(part[c, 0][:, t // 2, :], window)
-            else:
-                nc.vector.tensor_tensor(part[c, r][:, t // 2, :], window, part[c, r - 1][:, t // 2, :], ALU.add)
+            second[c, t] = dst
+            nc.vector.tensor_tensor(dst, spin[t][:].indirect(entries(1, j0, n)), first[:, t // 2, j0 : j0 + n], ALU.add)
+
+        def fetch_third(c, t):
+            j0, n = CHUNKS[c]
+            nc.vector.tensor_tensor(third[:, t // 2, j0 : j0 + n], spin[t][:].indirect(entries(2, j0, n)), second[c, t], ALU.add)
 
         def arg_vector(c, t):
             j0, n = CHUNKS[c]
-            h, i0 = divmod(j0, HALF)
-            nc.vector.tensor_tensor(arg[h][:, t, i0 : i0 + n], part[c, 2][:, t // 2, :], spin[t][:, j0 : j0 + n], ALU.mult)
+            nc.vector.tensor_tensor(arg[:, t // 2, j0 : j0 + n], third[:, t // 2, j0 : j0 + n], spin[t][:, j0 : j0 + n], ALU.mult)
 
-        def turn_vec_tiles(c):
+        def turn_vec_tiles(c, tiles):
             j0, n = CHUNKS[c]
-            h, i0 = divmod(j0, HALF)
-            nc.scalar.activation(th[h][:, 0::2, i0 : i0 + n], arg[h][:, 0::2, i0 : i0 + n], ACT.Tanh)
+            nc.scalar.activation(th[:, tiles[0] : tiles[-1] + 1 : 2, j0 : j0 + n], arg[:, tiles[0] // 2 : tiles[-1] // 2 + 1, j0 : j0 + n], ACT.Tanh)
 
         sig = {}
-        for c, (j0, n) in enumerate(CHUNKS):
-            for t in SCA_TILES:
-                for r in range(3):
-                    sig[c, t, r] = alloc("sig%d_%d_%d" % (c, t, r), [P, n], F32)
-        turned, turned_sb, field = {}, {}, {}
-
-        def fetch_scalar(c, t, r):
-            j0, n = CHUNKS[c]
-            nc.scalar.activation(sig[c, t, r][:], pre[t][:].indirect(entries(r, j0, n)), ACT.Sigmoid)
+        turned, arg_back = {}, {}
 
         def group_of(c, t):
             return SCA_TILES if c < 2 else (t,)
 
-        def rows(tiles):
-            return slice(tiles[0], tiles[-1] + 1, 2)
-
-        def sum_turned(c, t):
-            blocks = CHUNKS[c][1] // P
+        def fetch_scalar(c, t, slots):
+            j0, n = CHUNKS[c]
+            for r in range(3):
+                sig[c, t, r] = slots[r]
+                nc.scalar.activation(slots[r], pre[t][:].indirect(entries(r, j0, n)), ACT.Sigmoid)
             tiles = group_of(c, t)
             if t == tiles[0]:
-                turned[c, tiles] = ps.tile([P, len(tiles), blocks, P], F32, name="turned%d_%d" % (c, t), tag=TURN_BANKS[c, t][0])
-            for jb in range(blocks):
+                turned[c, tiles] = ps.tile([P, len(tiles), n // P, P], F32, name="turned%d_%d" % (c, t), tag=TURN_BANKS[c, t][0])
+            for jb in range(n // P):
                 for r in range(3):
                     nc.tensor.matmul(
-                        turned[c, tiles][:, tiles.index(t), jb, :], sig[c, t, r][:, jb * P : (jb + 1) * P], ident[:], start=(r == 0), stop=(r == 2), is_transpose=True
+                        turned[c, tiles][:, tiles.index(t), jb, :], slots[r][:, jb * P : (jb + 1) * P], ident[:], start=(r == 0), stop=(r == 2), is_transpose=True
                     )
 
-        def turn_back(c, tiles, on_vector):
-            blocks = CHUNKS[c][1] // P
-            staged = alloc("turned_sb%d_%d" % (c, tiles[0]), [P, len(tiles), blocks, P], F32)
-            if on_vector:
-                nc.vector.tensor_scalar(staged[:], turned[c, tiles][:], 2.0, None, ALU.mult)
-            else:
-                nc.scalar.activation(staged[:], turned[c, tiles][:], ACT.Copy, scale=2.0)
-            field[c, tiles] = ps.tile([P, len(tiles), blocks, P], F32, name="field%d_%d" % (c, tiles[0]), tag=TURN_BANKS[c, tiles[0]][1])
-            for b in range(len(tiles)):
-                for jb in range(blocks):
-                    nc.tensor.transpose(field[c, tiles][:, b, jb, :], staged[:, b, jb, :], ident[:])
-
-        def arg_sca_tiles(c, tiles):
+        def arg_turned(c, tiles):
             j0, n = CHUNKS[c]
-            h, i0 = divmod(j0, HALF)
+            name = "arg_turned%d_%d" % (c, tiles[0])
+            staged = sb.tile([P, len(tiles), n], F32, name=name, tag=name, align_bytes=64)
             nc.vector.scalar_tensor_tensor(
-                arg[h][:, rows(tiles), i0 : i0 + n],
-                field[c, tiles][:].rearrange("p b k j -> p b (k j)"),
-                -3.0,
-                spin_s[:, tiles[0] // 2 : tiles[-1] // 2 + 1, j0 : j0 + n],
+                staged[:],
+                turned[c, tiles][:].rearrange("j b k p -> j b (k p)"),
+                -1.5,
+                spin_turned[:, tiles[0] // 2 : tiles[-1] // 2 + 1, j0 // P : (j0 + n) // P, :].rearrange("j b k p -> j b (k p)"),
                 ALU.add,
                 ALU.mult,
             )
+            arg_back[c, tiles] = ps.tile([P, len(tiles), n], F32, name="arg_back%d_%d" % (c, tiles[0]), tag=TURN_BANKS[c, tiles[0]][1])
+            for b in range(len(tiles)):
+                for jb in range(n // P):
+                    nc.tensor.transpose(arg_back[c, tiles][:, b, jb * P : (jb + 1) * P], staged[:, b, jb * P : (jb + 1) * P], ident[:])
 
         def turn_sca_tiles(c, tiles):
             j0, n = CHUNKS[c]
-            h, i0 = divmod(j0, HALF)
-            nc.scalar.activation(th[h][:, rows(tiles), i0 : i0 + n], arg[h][:, rows(tiles), i0 : i0 + n], ACT.Tanh)
-
-        def fetch_tile_scalar(c, t):
-            for r in range(3):
-                fetch_scalar(c, t, r)
-            sum_turned(c, t)
+            nc.scalar.activation(th[:, tiles[0] : tiles[-1] + 1 : 2, j0 : j0 + n], arg_back[c, tiles][:], ACT.Tanh, scale=2.0)
 
         z_bf, z_codes, z_scales = {}, {}, {}
 
-        def make_z(c):
+        def make_z(c, dst):
             j0, n = CHUNKS[c]
-            h, i0 = divmod(j0, HALF)
-            z_bf[c] = alloc("z_bf%d" % c, [P, n, PACK], BF16)
+            z_bf[c] = dst
             nc.vector.tensor_tensor(
-                z_bf[c][:].rearrange("p (g i) t -> p g t i", i=RUN),
-                th[h][:, :, i0 : i0 + n].rearrange("p t (g i) -> p g t i", i=RUN),
+                dst.rearrange("p (g i t) -> p g t i", i=RUN, t=PACK),
+                th[:, :, j0 : j0 + n].rearrange("p t (g i) -> p g t i", i=RUN),
                 gy[:, :, j0 : j0 + n].rearrange("p t (g i) -> p g t i", i=RUN),
                 ALU.mult,
             )
@@ -243,7 +240,7 @@ def tile_picked_isingm_none_p_kernel(tc, x_words, x_scales, w1, gn, w2, offs, p1
             j0, n = CHUNKS[c]
             z_codes[c] = alloc("z_codes%d" % c, [P, n], U32)
             z_scales[c] = alloc("z_scales%d" % c, [P, n], U8)
-            nc.vector.quantize_mx(z_codes[c][:].bitcast(FP8X4), z_scales[c][:], z_bf[c][:].rearrange("p n t -> p (n t)"))
+            nc.vector.quantize_mx(z_codes[c][:].bitcast(FP8X4), z_scales[c][:], z_bf[c])
 
         w2_bf = {}
         w2_codes = alloc("w2_codes", [P, N], U32)
@@ -279,74 +276,80 @@ def tile_picked_isingm_none_p_kernel(tc, x_words, x_scales, w1, gn, w2, offs, p1
                         start=True,
                         stop=True,
                     )
-                res = alloc("res%d_%d" % (c, b), [P, per, n], F32)
+                name = "res%d_%d" % (c, b)
+                res = sb.tile([P, per, n], F32, name=name, tag=RES_TAGS.get((c, b), name), align_bytes=64)
                 copies[b](res[:], bank[:])
                 queues[b].dma_start(out_rows[:, b * per : (b + 1) * per, j0 : j0 + n], res[:])
 
+        early = alloc("early", [P, 2, 3, HALF], F32)
+        middle = alloc("middle", [P, 4, P], F32)
+        second0 = alloc("second0", [P, 2, HALF], F32)
+        z_first = alloc("z_first", [P, HALF * PACK], BF16)
+        z_last = alloc("z_last", [P, P * PACK], BF16)
+
         make_spin(0)
-        pre_vector(1)
+        make_pre(1, True)
+        turn_pre(1)
         cast_w2(nc.vector.tensor_copy, 0, 0, P, "w2_bf0")
         cast_w2(nc.scalar.copy, 0, P, P, "w2_bf0")
-        fetch_scalar(0, 1, 0)
         make_spin(2)
-        fetch_scalar(0, 1, 1)
-        fetch_scalar(0, 1, 2)
-        sum_turned(0, 1)
-        fetch_vector(0, 0, 0)
-        pre_vector(3)
-        fetch_vector(0, 1, 0)
-        make_gy(0)
-        fetch_vector(0, 2, 0)
-        fetch_vector(0, 0, 2)
+        fetch_scalar(0, 1, [early[:, 0, r, :] for r in range(3)])
+        fetch_first(0, 0, HALF)
+        make_pre(3, True)
+        turn_pre(3)
+        fetch_second(0, 0, second0[:, 0, :])
+        make_gy(0, True)
+        fetch_third(0, 0)
+        fetch_first(2, 0, HALF)
         arg_vector(0, 0)
-        fetch_vector(0, 1, 2)
+        fetch_second(0, 2, second0[:, 1, :])
         quant_w2(0)
-        fetch_vector(0, 2, 2)
-        make_gy(2)
+        fetch_third(0, 2)
+        make_gy(2, True)
         arg_vector(0, 2)
-        fetch_tile_scalar(0, 3)
-        spin_from_pre(1)
-        spin_from_pre(3)
-        turn_back(0, SCA_TILES, False)
-        fetch_tile_scalar(1, 1)
-        turn_vec_tiles(0)
-        arg_sca_tiles(0, SCA_TILES)
-        fetch_tile_scalar(1, 3)
+        make_spin_turned(1)
+        fetch_scalar(0, 3, [early[:, 1, r, :] for r in range(3)])
+        make_spin_turned(3)
+        arg_turned(0, SCA_TILES)
+        fetch_scalar(1, 1, [middle[:, r, :] for r in range(3)])
+        turn_vec_tiles(0, VEC_TILES)
+        make_gy(1, False)
+        make_gy(3, False)
         turn_sca_tiles(0, SCA_TILES)
-        for r in range(3):
-            for t in VEC_TILES:
-                fetch_vector(1, r, t)
-        make_gy(1)
-        make_gy(3)
-        turn_back(1, SCA_TILES, True)
-        fetch_tile_scalar(2, 1)
-        fetch_tile_scalar(2, 3)
-        make_z(0)
+        late = sb.tile([P, 8, P], F32, name="late", tag="arg_turned0_1", align_bytes=64)
+        fetch_scalar(1, 3, [middle[:, 3, :], late[:, 0, :], late[:, 1, :]])
+        for t in VEC_TILES:
+            fetch_first(t, HALF, HALF)
+        cast_w2(nc.vector.tensor_copy, 1, 0, 2 * P, "w2_bf1")
+        quant_w2(1)
+        fetch_second(1, 0, early[:, 1, 2, P:])
+        fetch_second(1, 2, early[:, 1, 2, :P])
+        for t in VEC_TILES:
+            fetch_third(1, t)
+        fetch_scalar(2, 1, [late[:, 2 + r, :] for r in range(3)])
         arg_vector(1, 0)
         arg_vector(1, 2)
+        make_z(0, z_first[:])
+        arg_turned(1, SCA_TILES)
+        fetch_scalar(2, 3, [late[:, 5 + r, :] for r in range(3)])
         quant_z(0)
-        arg_sca_tiles(1, SCA_TILES)
-        turn_back(2, (1,), False)
-        turn_vec_tiles(1)
-        turn_back(2, (3,), False)
+        turn_vec_tiles(1, VEC_TILES)
         turn_sca_tiles(1, SCA_TILES)
-        cast_w2(nc.scalar.copy, 1, 0, P, "pre1")
-        cast_w2(nc.scalar.copy, 1, P, P, "pre1")
-        for r in range(3):
-            for t in VEC_TILES:
-                fetch_vector(2, r, t)
-        arg_sca_tiles(2, (1,))
-        arg_vector(2, 0)
-        arg_vector(2, 2)
-        arg_sca_tiles(2, (3,))
-        turn_sca_tiles(2, (1,))
-        turn_vec_tiles(2)
-        turn_sca_tiles(2, (3,))
-        make_z(1)
-        quant_w2(1)
+        for t in VEC_TILES:
+            fetch_second(2, t, late[:, t // 2, :])
+        for t in VEC_TILES:
+            fetch_third(2, t)
+        for t in SCA_TILES:
+            arg_turned(2, (t,))
+        for t in VEC_TILES:
+            arg_vector(2, t)
+        for t in SCA_TILES:
+            turn_sca_tiles(2, (t,))
+            turn_vec_tiles(2, (t - 1,))
         product2(0, ("bank4", "bank5"), (nc.scalar.copy, nc.scalar.copy), (nc.sync, nc.sync))
+        make_z(1, late[:, 0:2, :].rearrange("p k j -> p (k j)").bitcast(BF16))
         quant_z(1)
-        product2(1, ("bank2",), (nc.scalar.copy,), (nc.sync,))
-        make_z(2)
+        product2(1, ("bank0",), (nc.scalar.copy,), (nc.sync,))
+        make_z(2, z_last[:])
         quant_z(2)
         product2(2, ("bank3", "bank6"), (nc.vector.tensor_copy, nc.scalar.copy), (nc.sync, nc.scalar))

@@ -18,14 +18,15 @@ ACT = mybir.ActivationFunctionType
 
 P = 128
 PACK = 4
+GROUP = 16
+LISTS = 3
 HALF = S // 2
 CHUNKS = ((0, 256), (256, 128), (384, 128))
-W1_VECTOR_COLS = 64
-VEC_TILES = (0, 2)
-SCA_TILES = (1, 3)
-TURN_BANKS = {(0, 1): ("bank0", "bank1"), (1, 1): ("bank2", "bank3"), (2, 1): ("bank6", "bank7"), (2, 3): ("bank2", "bank1")}
+LAST = len(CHUNKS) - 1
+VECTOR_TILES = (0, 2)
+SCALAR_TILES = (1, 3)
+W1_VECTOR = 64
 RUN = 2
-RES_TAGS = {(0, 1): "arg"}
 
 
 def tile_picked_isingm_none_p_kernel(tc, x_words, x_scales, w1, gn, w2, offs, p1, p2, p3, out):
@@ -34,21 +35,36 @@ def tile_picked_isingm_none_p_kernel(tc, x_words, x_scales, w1, gn, w2, offs, p1
         sb = ctx.enter_context(tc.tile_pool(name="sb", bufs=1))
         ps = ctx.enter_context(tc.psum_pool(name="ps", bufs=1))
 
-        def alloc(name, shape, dtype):
-            return sb.tile(shape, dtype, name=name, align_bytes=64)
+        def alloc(name, shape, dtype, tag=None):
+            return sb.tile(shape, dtype, name=name, tag=tag or name, align_bytes=64)
 
-        offs_sb = sb.tile([P, S // 16], U16, name="offs_sb")
-        lists = [sb.tile([P, S // 16], U16, name="list%d" % r) for r in range(3)]
+        def bank(name, shape, number):
+            return ps.tile(shape, F32, name=name, tag="bank%d" % number)
+
+        def product(dst, w_codes, w_scales, tile, codes, scales):
+            cols = slice(tile * P, (tile + 1) * P)
+            nc.tensor.matmul_mx(
+                out=dst,
+                lhsT=w_codes[:, cols].bitcast(FP8X4),
+                lhsT_scale=w_scales[:, cols],
+                rhs=codes.bitcast(FP8X4),
+                rhs_scale=scales,
+                start=True,
+                stop=True,
+            )
+
+        offs_sb = sb.tile([P, S // GROUP], U16, name="offs_sb")
+        lists = [sb.tile([P, S // GROUP], U16, name="list%d" % r) for r in range(LISTS)]
         xs_win = alloc("xs_win", [P, T], U8)
         xw_win = alloc("xw_win", [P, T], I32)
         w1_raw = alloc("w1_raw", [P, PACK, H], F32)
         gn_sb = alloc("gn_sb", [P, PACK], F32)
-        warm = alloc("warm", [P, 1], F32)
-        warm_out = alloc("warm_out", [P, 1], F32)
-
+        zero = alloc("zero", [P, 1], F32)
+        one_half = alloc("one_half", [P, 1], F32)
         xs_rows = alloc("xs_rows", [P, T // 4], I32)
-        for q in range(4):
-            (nc.scalar, nc.sync)[q % 2].dma_start(xs_rows[32 * q : 32 * q + 4, :], x_scales[0, 4 * q : 4 * q + 4, :].bitcast(I32))
+        scale_rows = [slice(32 * q, 32 * q + 4) for q in range(4)]
+        for q, rows in enumerate(scale_rows):
+            (nc.scalar, nc.sync)[q % 2].dma_start(xs_rows[rows, :], x_scales[0, 4 * q : 4 * q + 4, :].bitcast(I32))
         nc.scalar.dma_start(gn_sb[:], gn.rearrange("(p t) o -> p (t o)", t=PACK))
         nc.sync.dma_start(offs_sb[:], offs)
         nc.sync.dma_start(w1_raw[:], w1.rearrange("(p j) c -> p j c", j=PACK))
@@ -59,170 +75,147 @@ def tile_picked_isingm_none_p_kernel(tc, x_words, x_scales, w1, gn, w2, offs, p1
         for h in range(2):
             nc.sync.dma_start(w2_raw[h][:], w2.rearrange("(p j) c -> p j c", j=PACK)[:, :, h * (N // 2) : (h + 1) * (N // 2)])
 
-        nc.gpsimd.memset(warm[:], 0.0)
-        nc.scalar.activation(warm_out[:], warm[:], ACT.Sigmoid)
+        nc.gpsimd.memset(zero[:], 0.0)
+        nc.scalar.activation(one_half[:], zero[:], ACT.Sigmoid)
         ident = alloc("ident", [P, P], F32)
         make_identity(nc, ident[:])
+
         nc.vector.memset(xs_win[:].bitcast(I32), 0)
-        for q in range(4):
-            nc.vector.tensor_copy(xs_win[32 * q : 32 * q + 4, :].bitcast(I32), xs_rows[32 * q : 32 * q + 4, :])
+        for rows in scale_rows:
+            nc.vector.tensor_copy(xs_win[rows, :].bitcast(I32), xs_rows[rows, :])
         xs = alloc("xs", [P, S], U8)
         nc.vector.tensor_copy(xs[:], xs_win[:].indirect(offs_sb[:]))
 
         w1_bf = alloc("w1_bf", [P, PACK, P, PACK], BF16)
         w1_src = w1_raw[:].rearrange("p j (m t) -> p m j t", t=PACK)
         w1_dst = w1_bf[:].rearrange("p t m j -> p m j t")
-        nc.vector.tensor_copy(w1_dst[:, :W1_VECTOR_COLS], w1_src[:, :W1_VECTOR_COLS])
-        nc.scalar.copy(w1_dst[:, W1_VECTOR_COLS:], w1_src[:, W1_VECTOR_COLS:])
-
+        nc.vector.tensor_copy(w1_dst[:, :W1_VECTOR], w1_src[:, :W1_VECTOR])
+        nc.scalar.copy(w1_dst[:, W1_VECTOR:], w1_src[:, W1_VECTOR:])
         w1_codes = alloc("w1_codes", [P, H], U32)
         w1_scales = alloc("w1_scales", [P, H], U8)
 
-        def quant_w1(t0):
+        def quantise_w1(t0):
             cols = slice(t0 * P, (t0 + 2) * P)
             nc.vector.quantize_mx(w1_codes[:, cols].bitcast(FP8X4), w1_scales[:, cols], w1_bf[:, t0 : t0 + 2].rearrange("p t m j -> p (t m j)"))
 
-        quant_w1(0)
+        quantise_w1(0)
 
-        banks = {}
-        for t in range(2):
-            for h in range(2):
-                banks[t, h] = ps.tile([P, HALF], F32, name="a%d%d" % (t, h), tag="bank%d" % (2 * t + h))
-        full = {}
+        halves = [slice(h * HALF, (h + 1) * HALF) for h in range(2)]
+        a_parts = {t: [(bank("a%d%d" % (t, h), [P, HALF], 2 * t + h), halves[h]) for h in range(2)] for t in range(2)}
         for t in range(2, PACK):
-            full[t] = ps.tile([P, S], F32, name="a%d" % t, tag="bank%d" % (t + 2))
+            a_parts[t] = [(bank("a%d" % t, [P, S], t + 2), slice(0, S))]
         xw = alloc("xw", [P, S], U32)
-        for h in range(2):
-            nc.vector.tensor_copy(xw[:, h * HALF : (h + 1) * HALF], xw_win[:].bitcast(U32).indirect(offs_sb[:, h * 16 : (h + 1) * 16]))
-        quant_w1(2)
+        for cols in halves:
+            nc.vector.tensor_copy(xw[:, cols], xw_win[:].bitcast(U32).indirect(offs_sb[:, cols.start // GROUP : cols.stop // GROUP]))
+        quantise_w1(2)
+        for t, h in ((0, 0), (1, 0), (0, 1), (1, 1), (2, 0), (3, 0)):
+            dst, cols = a_parts[t][h]
+            product(dst[:], w1_codes, w1_scales, t, xw[:, cols], xs[:, cols])
 
-        def product1(dst, t, cols):
-            nc.tensor.matmul_mx(
-                out=dst,
-                lhsT=w1_codes[:, t * P : (t + 1) * P].bitcast(FP8X4),
-                lhsT_scale=w1_scales[:, t * P : (t + 1) * P],
-                rhs=xw[:, cols].bitcast(FP8X4),
-                rhs_scale=xs[:, cols],
-                start=True,
-                stop=True,
-            )
-
-        for h in range(2):
-            for t in range(2):
-                product1(banks[t, h][:], t, slice(h * HALF, (h + 1) * HALF))
-        for t in range(2, PACK):
-            product1(full[t][:], t, slice(0, S))
-
-        spin = {t: alloc("spin%d" % t, [P, S], F32) for t in VEC_TILES}
-        pre = {t: sb.tile([P, S], F32, name="pre%d" % t, tag="pre%d" % t, align_bytes=64) for t in SCA_TILES}
-        spin_turned = alloc("spin_turned", [P, 2, S // P, P], F32)
+        y = {t: alloc("y%d" % t, [P, S], F32) for t in VECTOR_TILES}
+        a2 = {t: alloc("a2_%d" % t, [P, S], F32) for t in SCALAR_TILES}
+        y_turned = alloc("y_turned", [P, 2, S // P, P], F32)
         gy = alloc("gy", [P, PACK, S], F32)
+        a2_turned, y_back = {}, {}
 
-        def pieces(t):
-            if t < 2:
-                return [(banks[t, h][:], slice(h * HALF, (h + 1) * HALF)) for h in range(2)]
-            return [(full[t][:], slice(0, S))]
+        def make_y(t):
+            for src, cols in a_parts[t]:
+                nc.scalar.activation(y[t][:, cols], src[:], ACT.Tanh)
 
-        def make_spin(t):
-            for src, cols in pieces(t):
-                nc.scalar.activation(spin[t][:, cols], src, ACT.Tanh)
-
-        def make_pre(t, on_vector):
-            for src, cols in pieces(t):
-                if on_vector:
-                    nc.vector.tensor_scalar(pre[t][:, cols], src, 2.0, None, ALU.mult)
-                else:
-                    nc.scalar.activation(pre[t][:, cols], src, ACT.Copy, scale=2.0)
-
-        pre_turned, spin_back = {}, {}
-
-        def turn_pre(t):
-            pre_turned[t] = ps.tile([P, S // P, P], F32, name="pre_turned%d" % t, tag="bank%d" % (6 + t // 2))
+        def make_a2(t):
+            for src, cols in a_parts[t]:
+                nc.vector.tensor_scalar(a2[t][:, cols], src[:], 2.0, None, ALU.mult)
+            a2_turned[t] = bank("a2_turned%d" % t, [P, S // P, P], 6 + t // 2)
             for jb in range(S // P):
-                nc.tensor.transpose(pre_turned[t][:, jb, :], pre[t][:, jb * P : (jb + 1) * P], ident[:])
+                nc.tensor.transpose(a2_turned[t][:, jb, :], a2[t][:, jb * P : (jb + 1) * P], ident[:])
 
-        def make_spin_turned(t):
-            nc.scalar.activation(spin_turned[:, t // 2], pre_turned[t][:], ACT.Tanh, scale=0.5)
-            spin_back[t] = ps.tile([P, S // P, P], F32, name="spin_back%d" % t, tag="bank%d" % (4 + t // 2))
+        def make_y_turned(t):
+            nc.scalar.activation(y_turned[:, t // 2], a2_turned[t][:], ACT.Tanh, scale=one_half[:, 0:1])
+            y_back[t] = bank("y_back%d" % t, [P, S // P, P], 4 + t // 2)
             for jb in range(S // P):
-                nc.tensor.transpose(spin_back[t][:, jb, :], spin_turned[:, t // 2, jb, :], ident[:])
+                nc.tensor.transpose(y_back[t][:, jb, :], y_turned[:, t // 2, jb, :], ident[:])
 
-        def make_gy(t, on_vector):
-            src = spin[t][:] if t in VEC_TILES else spin_back[t][:].rearrange("p k j -> p (k j)")
-            if on_vector:
-                nc.vector.tensor_scalar(gy[:, t, :], src, gn_sb[:, t : t + 1], None, ALU.mult)
+        def make_gy(t):
+            gain = gn_sb[:, t : t + 1]
+            if t in VECTOR_TILES:
+                nc.vector.tensor_scalar(gy[:, t, :], y[t][:], gain, None, ALU.mult)
             else:
-                nc.scalar.activation(gy[:, t, :], src, ACT.Copy, scale=gn_sb[:, t : t + 1])
+                nc.scalar.activation(gy[:, t, :], y_back[t][:].rearrange("p k j -> p (k j)"), ACT.Copy, scale=gain)
 
         def entries(r, j0, n):
-            return lists[r][:, j0 // 16 : (j0 + n) // 16]
+            return lists[r][:, j0 // GROUP : (j0 + n) // GROUP]
 
-        first = alloc("first", [P, 2, S], F32)
-        third = alloc("third", [P, 2, S], F32)
-        second = {}
-        arg = sb.tile([P, 2, S], F32, name="arg", tag="arg", align_bytes=64)
-        th = alloc("th", [P, PACK, S], F32)
+        def feature_tiles(tiles):
+            return slice(tiles[0], tiles[-1] + 1, 2)
 
-        def fetch_first(t, j0, n):
-            nc.vector.tensor_copy(first[:, t // 2, j0 : j0 + n], spin[t][:].indirect(entries(0, j0, n)))
+        def own_tiles(tiles):
+            return slice(tiles[0] // 2, tiles[-1] // 2 + 1)
+
+        y1 = alloc("y1", [P, 2, S], F32)
+        fl = alloc("fl", [P, 2, S], F32)
+        y12 = {}
+        u = alloc("u", [P, 2, S], F32)
+        tanh_u = alloc("tanh_u", [P, PACK, S], F32)
+
+        def fetch_first(t, cols):
+            nc.vector.tensor_copy(y1[:, t // 2, cols], y[t][:].indirect(entries(0, cols.start, cols.stop - cols.start)))
 
         def fetch_second(c, t, dst):
             j0, n = CHUNKS[c]
-            second[c, t] = dst
-            nc.vector.tensor_tensor(dst, spin[t][:].indirect(entries(1, j0, n)), first[:, t // 2, j0 : j0 + n], ALU.add)
+            y12[c, t] = dst
+            nc.vector.tensor_tensor(dst, y[t][:].indirect(entries(1, j0, n)), y1[:, t // 2, j0 : j0 + n], ALU.add)
 
         def fetch_third(c, t):
             j0, n = CHUNKS[c]
-            nc.vector.tensor_tensor(third[:, t // 2, j0 : j0 + n], spin[t][:].indirect(entries(2, j0, n)), second[c, t], ALU.add)
+            nc.vector.tensor_tensor(fl[:, t // 2, j0 : j0 + n], y[t][:].indirect(entries(2, j0, n)), y12[c, t], ALU.add)
 
-        def arg_vector(c, t):
+        def make_u(c, t):
             j0, n = CHUNKS[c]
-            nc.vector.tensor_tensor(arg[:, t // 2, j0 : j0 + n], third[:, t // 2, j0 : j0 + n], spin[t][:, j0 : j0 + n], ALU.mult)
+            nc.vector.tensor_tensor(u[:, t // 2, j0 : j0 + n], fl[:, t // 2, j0 : j0 + n], y[t][:, j0 : j0 + n], ALU.mult)
 
-        def turn_vec_tiles(c, tiles):
+        def tanh_of_u(c, tiles):
             j0, n = CHUNKS[c]
-            nc.scalar.activation(th[:, tiles[0] : tiles[-1] + 1 : 2, j0 : j0 + n], arg[:, tiles[0] // 2 : tiles[-1] // 2 + 1, j0 : j0 + n], ACT.Tanh)
+            nc.scalar.activation(tanh_u[:, feature_tiles(tiles), j0 : j0 + n], u[:, own_tiles(tiles), j0 : j0 + n], ACT.Tanh)
 
-        sig = {}
-        turned, arg_back = {}, {}
+        sums, half_u = {}, {}
 
-        def group_of(c, t):
-            return SCA_TILES if c < 2 else (t,)
+        def open_sums(c, tiles, number):
+            sums[c, tiles] = bank("sums%d_%d" % (c, tiles[0]), [P, len(tiles), CHUNKS[c][1] // P, P], number)
 
-        def fetch_scalar(c, t, slots):
+        def fetch_and_add(c, tiles, t, dsts):
             j0, n = CHUNKS[c]
-            for r in range(3):
-                sig[c, t, r] = slots[r]
-                nc.scalar.activation(slots[r], pre[t][:].indirect(entries(r, j0, n)), ACT.Sigmoid)
-            tiles = group_of(c, t)
-            if t == tiles[0]:
-                turned[c, tiles] = ps.tile([P, len(tiles), n // P, P], F32, name="turned%d_%d" % (c, t), tag=TURN_BANKS[c, t][0])
+            for r in range(LISTS):
+                nc.scalar.activation(dsts[r], a2[t][:].indirect(entries(r, j0, n)), ACT.Sigmoid)
             for jb in range(n // P):
-                for r in range(3):
+                for r in range(LISTS):
                     nc.tensor.matmul(
-                        turned[c, tiles][:, tiles.index(t), jb, :], slots[r][:, jb * P : (jb + 1) * P], ident[:], start=(r == 0), stop=(r == 2), is_transpose=True
+                        sums[c, tiles][:, tiles.index(t), jb, :],
+                        dsts[r][:, jb * P : (jb + 1) * P],
+                        ident[:],
+                        start=(r == 0),
+                        stop=(r == LISTS - 1),
+                        is_transpose=True,
                     )
 
-        def arg_turned(c, tiles):
+        def make_half_u(c, tiles, number):
             j0, n = CHUNKS[c]
-            name = "arg_turned%d_%d" % (c, tiles[0])
-            staged = sb.tile([P, len(tiles), n], F32, name=name, tag=name, align_bytes=64)
+            turned = alloc("half_u_turned%d_%d" % (c, tiles[0]), [P, len(tiles), n], F32)
             nc.vector.scalar_tensor_tensor(
-                staged[:],
-                turned[c, tiles][:].rearrange("j b k p -> j b (k p)"),
-                -1.5,
-                spin_turned[:, tiles[0] // 2 : tiles[-1] // 2 + 1, j0 // P : (j0 + n) // P, :].rearrange("j b k p -> j b (k p)"),
+                turned[:],
+                sums[c, tiles][:].rearrange("j b k p -> j b (k p)"),
+                -LISTS / 2,
+                y_turned[:, own_tiles(tiles), j0 // P : (j0 + n) // P, :].rearrange("j b k p -> j b (k p)"),
                 ALU.add,
                 ALU.mult,
             )
-            arg_back[c, tiles] = ps.tile([P, len(tiles), n], F32, name="arg_back%d_%d" % (c, tiles[0]), tag=TURN_BANKS[c, tiles[0]][1])
+            half_u[c, tiles] = bank("half_u%d_%d" % (c, tiles[0]), [P, len(tiles), n], number)
             for b in range(len(tiles)):
                 for jb in range(n // P):
-                    nc.tensor.transpose(arg_back[c, tiles][:, b, jb * P : (jb + 1) * P], staged[:, b, jb * P : (jb + 1) * P], ident[:])
+                    nc.tensor.transpose(half_u[c, tiles][:, b, jb * P : (jb + 1) * P], turned[:, b, jb * P : (jb + 1) * P], ident[:])
 
-        def turn_sca_tiles(c, tiles):
+        def tanh_of_half_u(c, tiles):
             j0, n = CHUNKS[c]
-            nc.scalar.activation(th[:, tiles[0] : tiles[-1] + 1 : 2, j0 : j0 + n], arg_back[c, tiles][:], ACT.Tanh, scale=2.0)
+            nc.scalar.activation(tanh_u[:, feature_tiles(tiles), j0 : j0 + n], half_u[c, tiles][:], ACT.Tanh, scale=2.0)
 
         z_bf, z_codes, z_scales = {}, {}, {}
 
@@ -231,13 +224,13 @@ def tile_picked_isingm_none_p_kernel(tc, x_words, x_scales, w1, gn, w2, offs, p1
             z_bf[c] = dst
             nc.vector.tensor_tensor(
                 dst.rearrange("p (g i t) -> p g t i", i=RUN, t=PACK),
-                th[:, :, j0 : j0 + n].rearrange("p t (g i) -> p g t i", i=RUN),
+                tanh_u[:, :, j0 : j0 + n].rearrange("p t (g i) -> p g t i", i=RUN),
                 gy[:, :, j0 : j0 + n].rearrange("p t (g i) -> p g t i", i=RUN),
                 ALU.mult,
             )
 
-        def quant_z(c):
-            j0, n = CHUNKS[c]
+        def quantise_z(c):
+            n = CHUNKS[c][1]
             z_codes[c] = alloc("z_codes%d" % c, [P, n], U32)
             z_scales[c] = alloc("z_scales%d" % c, [P, n], U8)
             nc.vector.quantize_mx(z_codes[c][:].bitcast(FP8X4), z_scales[c][:], z_bf[c])
@@ -246,110 +239,104 @@ def tile_picked_isingm_none_p_kernel(tc, x_words, x_scales, w1, gn, w2, offs, p1
         w2_codes = alloc("w2_codes", [P, N], U32)
         w2_scales = alloc("w2_scales", [P, N], U8)
 
-        def cast_w2(copy, h, i0, n, tag):
-            if i0 == 0:
-                w2_bf[h] = sb.tile([P, N // 2, PACK], BF16, name="w2_bf%d" % h, tag=tag, align_bytes=64)
-            copy(
-                w2_bf[h][:, i0 : i0 + n, :].rearrange("p (g i) t -> p g t i", i=RUN),
-                w2_raw[h][:, :, i0 : i0 + n].rearrange("p t (g i) -> p g t i", i=RUN),
-            )
+        def cast_w2(copy, h, cols):
+            copy(w2_bf[h][:, cols, :].rearrange("p (g i) t -> p g t i", i=RUN), w2_raw[h][:, :, cols].rearrange("p t (g i) -> p g t i", i=RUN))
 
-        def quant_w2(h):
+        def quantise_w2(h):
             cols = slice(h * (N // 2), (h + 1) * (N // 2))
             nc.vector.quantize_mx(w2_codes[:, cols].bitcast(FP8X4), w2_scales[:, cols], w2_bf[h][:].rearrange("p n t -> p (n t)"))
 
         out_rows = out.rearrange("(m p) j -> p m j", p=P)
 
-        def product2(c, tags, copies, queues):
+        def product_out(c, m0, count, number, copy, queue, tag=None):
             j0, n = CHUNKS[c]
-            per = PACK // len(tags)
-            for b, tag in enumerate(tags):
-                bank = ps.tile([P, per, n], F32, name="o%d_%d" % (c, b), tag=tag)
-                for m in range(per):
-                    cols = slice((b * per + m) * P, (b * per + m + 1) * P)
-                    nc.tensor.matmul_mx(
-                        out=bank[:, m, :],
-                        lhsT=w2_codes[:, cols].bitcast(FP8X4),
-                        lhsT_scale=w2_scales[:, cols],
-                        rhs=z_codes[c][:].bitcast(FP8X4),
-                        rhs_scale=z_scales[c][:],
-                        start=True,
-                        stop=True,
-                    )
-                name = "res%d_%d" % (c, b)
-                res = sb.tile([P, per, n], F32, name=name, tag=RES_TAGS.get((c, b), name), align_bytes=64)
-                copies[b](res[:], bank[:])
-                queues[b].dma_start(out_rows[:, b * per : (b + 1) * per, j0 : j0 + n], res[:])
+            acc = bank("acc%d_%d" % (c, m0), [P, count, n], number)
+            for m in range(count):
+                product(acc[:, m, :], w2_codes, w2_scales, m0 + m, z_codes[c][:], z_scales[c][:])
+            res = alloc("res%d_%d" % (c, m0), [P, count, n], F32, tag)
+            copy(res[:], acc[:])
+            queue.dma_start(out_rows[:, m0 : m0 + count, j0 : j0 + n], res[:])
 
-        early = alloc("early", [P, 2, 3, HALF], F32)
-        middle = alloc("middle", [P, 4, P], F32)
-        second0 = alloc("second0", [P, 2, HALF], F32)
+        s_first = alloc("s_first", [P, 2, LISTS, HALF], F32)
+        s_second = alloc("s_second", [P, LISTS + 1, P], F32)
+        y12_first = alloc("y12_first", [P, 2, HALF], F32)
         z_first = alloc("z_first", [P, HALF * PACK], BF16)
         z_last = alloc("z_last", [P, P * PACK], BF16)
 
-        make_spin(0)
-        make_pre(1, True)
-        turn_pre(1)
-        cast_w2(nc.vector.tensor_copy, 0, 0, P, "w2_bf0")
-        cast_w2(nc.scalar.copy, 0, P, P, "w2_bf0")
-        make_spin(2)
-        fetch_scalar(0, 1, [early[:, 0, r, :] for r in range(3)])
-        fetch_first(0, 0, HALF)
-        make_pre(3, True)
-        turn_pre(3)
-        fetch_second(0, 0, second0[:, 0, :])
-        make_gy(0, True)
+        make_y(0)
+        make_a2(1)
+        w2_bf[0] = alloc("w2_bf0", [P, N // 2, PACK], BF16)
+        cast_w2(nc.vector.tensor_copy, 0, slice(0, P))
+        cast_w2(nc.scalar.copy, 0, slice(P, 2 * P))
+        make_y(2)
+        open_sums(0, SCALAR_TILES, 0)
+        fetch_and_add(0, SCALAR_TILES, 1, [s_first[:, 0, r, :] for r in range(LISTS)])
+        fetch_first(0, halves[0])
+        make_a2(3)
+        fetch_second(0, 0, y12_first[:, 0, :])
+        make_gy(0)
         fetch_third(0, 0)
-        fetch_first(2, 0, HALF)
-        arg_vector(0, 0)
-        fetch_second(0, 2, second0[:, 1, :])
-        quant_w2(0)
+        fetch_first(2, halves[0])
+        make_u(0, 0)
+        fetch_second(0, 2, y12_first[:, 1, :])
+        quantise_w2(0)
         fetch_third(0, 2)
-        make_gy(2, True)
-        arg_vector(0, 2)
-        make_spin_turned(1)
-        fetch_scalar(0, 3, [early[:, 1, r, :] for r in range(3)])
-        make_spin_turned(3)
-        arg_turned(0, SCA_TILES)
-        fetch_scalar(1, 1, [middle[:, r, :] for r in range(3)])
-        turn_vec_tiles(0, VEC_TILES)
-        make_gy(1, False)
-        make_gy(3, False)
-        turn_sca_tiles(0, SCA_TILES)
-        late = sb.tile([P, 8, P], F32, name="late", tag="arg_turned0_1", align_bytes=64)
-        fetch_scalar(1, 3, [middle[:, 3, :], late[:, 0, :], late[:, 1, :]])
-        for t in VEC_TILES:
-            fetch_first(t, HALF, HALF)
-        cast_w2(nc.vector.tensor_copy, 1, 0, 2 * P, "w2_bf1")
-        quant_w2(1)
-        fetch_second(1, 0, early[:, 1, 2, P:])
-        fetch_second(1, 2, early[:, 1, 2, :P])
-        for t in VEC_TILES:
+        make_gy(2)
+        make_u(0, 2)
+        make_y_turned(1)
+        fetch_and_add(0, SCALAR_TILES, 3, [s_first[:, 1, r, :] for r in range(LISTS)])
+        make_y_turned(3)
+        make_half_u(0, SCALAR_TILES, 1)
+
+        open_sums(1, SCALAR_TILES, 0)
+        fetch_and_add(1, SCALAR_TILES, 1, [s_second[:, r, :] for r in range(LISTS)])
+        tanh_of_u(0, VECTOR_TILES)
+        for t in SCALAR_TILES:
+            make_gy(t)
+        tanh_of_half_u(0, SCALAR_TILES)
+        s_late = alloc("s_late", [P, 2 + 2 * LISTS, P], F32, "half_u_turned0_1")
+        fetch_and_add(1, SCALAR_TILES, 3, [s_second[:, LISTS, :], s_late[:, 0, :], s_late[:, 1, :]])
+        for t in VECTOR_TILES:
+            fetch_first(t, halves[1])
+        w2_bf[1] = alloc("w2_bf1", [P, N // 2, PACK], BF16)
+        cast_w2(nc.vector.tensor_copy, 1, slice(0, N // 2))
+        quantise_w2(1)
+        fetch_second(1, 0, s_first[:, 1, LISTS - 1, P:])
+        fetch_second(1, 2, s_first[:, 1, LISTS - 1, :P])
+        for t in VECTOR_TILES:
             fetch_third(1, t)
-        fetch_scalar(2, 1, [late[:, 2 + r, :] for r in range(3)])
-        arg_vector(1, 0)
-        arg_vector(1, 2)
+
+        open_sums(LAST, (1,), 6)
+        fetch_and_add(LAST, (1,), 1, [s_late[:, 2 + r, :] for r in range(LISTS)])
+        for t in VECTOR_TILES:
+            make_u(1, t)
         make_z(0, z_first[:])
-        arg_turned(1, SCA_TILES)
-        fetch_scalar(2, 3, [late[:, 5 + r, :] for r in range(3)])
-        quant_z(0)
-        turn_vec_tiles(1, VEC_TILES)
-        turn_sca_tiles(1, SCA_TILES)
-        for t in VEC_TILES:
-            fetch_second(2, t, late[:, t // 2, :])
-        for t in VEC_TILES:
-            fetch_third(2, t)
-        for t in SCA_TILES:
-            arg_turned(2, (t,))
-        for t in VEC_TILES:
-            arg_vector(2, t)
-        for t in SCA_TILES:
-            turn_sca_tiles(2, (t,))
-            turn_vec_tiles(2, (t - 1,))
-        product2(0, ("bank4", "bank5"), (nc.scalar.copy, nc.scalar.copy), (nc.sync, nc.sync))
-        make_z(1, late[:, 0:2, :].rearrange("p k j -> p (k j)").bitcast(BF16))
-        quant_z(1)
-        product2(1, ("bank0",), (nc.scalar.copy,), (nc.sync,))
-        make_z(2, z_last[:])
-        quant_z(2)
-        product2(2, ("bank3", "bank6"), (nc.vector.tensor_copy, nc.scalar.copy), (nc.sync, nc.scalar))
+        make_half_u(1, SCALAR_TILES, 3)
+        open_sums(LAST, (3,), 0)
+        fetch_and_add(LAST, (3,), 3, [s_late[:, 2 + LISTS + r, :] for r in range(LISTS)])
+        quantise_z(0)
+        tanh_of_u(1, VECTOR_TILES)
+        tanh_of_half_u(1, SCALAR_TILES)
+        for t in VECTOR_TILES:
+            fetch_second(LAST, t, s_late[:, t // 2, :])
+        for t in VECTOR_TILES:
+            fetch_third(LAST, t)
+        make_half_u(LAST, (1,), 7)
+        make_half_u(LAST, (3,), 1)
+        for t in VECTOR_TILES:
+            make_u(LAST, t)
+        tanh_of_half_u(LAST, (1,))
+        for t in VECTOR_TILES:
+            tanh_of_u(LAST, (t,))
+        tanh_of_half_u(LAST, (3,))
+
+        product_out(0, 0, 2, 4, nc.scalar.copy, nc.sync)
+        product_out(0, 2, 2, 5, nc.scalar.copy, nc.sync, "u")
+        make_z(1, s_late[:, 0:2, :].rearrange("p k j -> p (k j)").bitcast(BF16))
+        quantise_z(1)
+        product_out(1, 0, 2, 0, nc.scalar.copy, nc.sync)
+        product_out(1, 2, 2, 2, nc.scalar.copy, nc.sync)
+        make_z(LAST, z_last[:])
+        quantise_z(LAST)
+        for m, number in enumerate((3, 6, 7, 1)):
+            product_out(LAST, m, 1, number, (nc.vector.tensor_copy, nc.scalar.copy)[m % 2], nc.scalar if m == PACK - 1 else nc.sync)

@@ -115,16 +115,19 @@ def tile_picked_isingm_none_p_kernel(tc, x_words, x_scales, w1, gn, w2, offs, p1
         y = {t: alloc("y%d" % t, [P, S], F32) for t in VECTOR_TILES}
         a2 = {t: alloc("a2_%d" % t, [P, S], F32) for t in SCALAR_TILES}
         y_turned = alloc("y_turned", [P, 2, S // P, P], F32)
-        gy = alloc("gy", [P, PACK, S], F32)
+        gy_y1 = alloc("gy_y1", [P, PACK + 2, S], F32, "w2_raw0")
+        gy = gy_y1[:, :PACK]
         a2_turned, y_back = {}, {}
 
-        def make_y(t):
-            for src, cols in a_parts[t]:
-                nc.scalar.activation(y[t][:, cols], src[:], ACT.Tanh)
+        def make_y(t, part):
+            src, cols = a_parts[t][part]
+            nc.scalar.activation(y[t][:, cols], src[:], ACT.Tanh)
 
-        def make_a2(t):
-            for src, cols in a_parts[t]:
-                nc.vector.tensor_scalar(a2[t][:, cols], src[:], 2.0, None, ALU.mult)
+        def make_a2(t, part):
+            src, cols = a_parts[t][part]
+            nc.scalar.activation(a2[t][:, cols], src[:], ACT.Copy, scale=2.0)
+
+        def turn_a2(t):
             a2_turned[t] = bank("a2_turned%d" % t, [P, S // P, P], 6 + t // 2)
             for jb in range(S // P):
                 nc.tensor.transpose(a2_turned[t][:, jb, :], a2[t][:, jb * P : (jb + 1) * P], ident[:])
@@ -151,7 +154,7 @@ def tile_picked_isingm_none_p_kernel(tc, x_words, x_scales, w1, gn, w2, offs, p1
         def own_tiles(tiles):
             return slice(tiles[0] // 2, tiles[-1] // 2 + 1)
 
-        y1 = alloc("y1", [P, 2, S], F32)
+        y1 = gy_y1[:, PACK:]
         fl = alloc("fl", [P, 2, S], F32)
         y12 = {}
         u = alloc("u", [P, 2, S], F32)
@@ -263,16 +266,18 @@ def tile_picked_isingm_none_p_kernel(tc, x_words, x_scales, w1, gn, w2, offs, p1
         z_first = alloc("z_first", [P, HALF * PACK], BF16)
         z_last = alloc("z_last", [P, P * PACK], BF16)
 
-        make_y(0)
-        make_a2(1)
         w2_bf[0] = alloc("w2_bf0", [P, N // 2, PACK], BF16)
-        cast_w2(nc.vector.tensor_copy, 0, slice(0, P))
-        cast_w2(nc.scalar.copy, 0, slice(P, 2 * P))
-        make_y(2)
+        cast_w2(nc.vector.tensor_copy, 0, slice(0, N // 2))
+        for h in range(2):
+            make_y(0, h)
+            make_a2(1, h)
+        turn_a2(1)
+        make_y(2, 0)
         open_sums(0, SCALAR_TILES, 0)
         fetch_and_add(0, SCALAR_TILES, 1, [s_first[:, 0, r, :] for r in range(LISTS)])
+        make_a2(3, 0)
+        turn_a2(3)
         fetch_first(0, halves[0])
-        make_a2(3)
         fetch_second(0, 0, y12_first[:, 0, :])
         make_gy(0)
         fetch_third(0, 0)
@@ -286,6 +291,8 @@ def tile_picked_isingm_none_p_kernel(tc, x_words, x_scales, w1, gn, w2, offs, p1
         make_y_turned(1)
         fetch_and_add(0, SCALAR_TILES, 3, [s_first[:, 1, r, :] for r in range(LISTS)])
         make_y_turned(3)
+        for t in VECTOR_TILES:
+            fetch_first(t, halves[1])
         make_half_u(0, SCALAR_TILES, 1)
 
         open_sums(1, SCALAR_TILES, 0)
@@ -296,8 +303,6 @@ def tile_picked_isingm_none_p_kernel(tc, x_words, x_scales, w1, gn, w2, offs, p1
         tanh_of_half_u(0, SCALAR_TILES)
         s_late = alloc("s_late", [P, 2 + 2 * LISTS, P], F32, "half_u_turned0_1")
         fetch_and_add(1, SCALAR_TILES, 3, [s_second[:, LISTS, :], s_late[:, 0, :], s_late[:, 1, :]])
-        for t in VECTOR_TILES:
-            fetch_first(t, halves[1])
         w2_bf[1] = alloc("w2_bf1", [P, N // 2, PACK], BF16)
         cast_w2(nc.vector.tensor_copy, 1, slice(0, N // 2))
         quantise_w2(1)

@@ -26,7 +26,7 @@ LAST = len(CHUNKS) - 1
 VECTOR_TILES = (0, 2)
 SCALAR_TILES = (1, 3)
 W1_VECTOR = 64
-RUN = 2
+RUN = 4
 
 
 def tile_picked_isingm_none_p_kernel(tc, x_words, x_scales, w1, gn, w2, offs, p1, p2, p3, out):

@@ -27,16 +27,23 @@ VECTOR_TILES = (0, 2)
 SCALAR_TILES = (1, 3)
 W1_VECTOR = 64
 RUN = 4
+SCALE_ROWS = K // 32
+W2_HALF_BYTES = PACK * (N // 2) * 4
+W2_SECOND = (PACK + 2) * S * 4
 
 
 def tile_picked_isingm_none_p_kernel(tc, x_words, x_scales, w1, gn, w2, offs, p1, p2, p3, out):
     nc = tc.nc
     with ExitStack() as ctx:
         sb = ctx.enter_context(tc.tile_pool(name="sb", bufs=1))
+        shared = ctx.enter_context(tc.tile_pool(name="shared", bufs=1))
         ps = ctx.enter_context(tc.psum_pool(name="ps", bufs=1))
 
         def alloc(name, shape, dtype, tag=None):
             return sb.tile(shape, dtype, name=name, tag=tag or name, align_bytes=64)
+
+        def place(name, shape, dtype, offset):
+            return shared.tile(shape, dtype, name=name, align_bytes=64, offset=offset)
 
         def bank(name, shape, number):
             return ps.tile(shape, F32, name=name, tag="bank%d" % number)
@@ -55,25 +62,20 @@ def tile_picked_isingm_none_p_kernel(tc, x_words, x_scales, w1, gn, w2, offs, p1
 
         offs_sb = sb.tile([P, S // GROUP], U16, name="offs_sb")
         lists = [sb.tile([P, S // GROUP], U16, name="list%d" % r) for r in range(LISTS)]
-        xs_win = alloc("xs_win", [P, T], U8)
+        xs_win = place("xs_win", [P, T], U8, W2_SECOND - T // 2)
         xw_win = alloc("xw_win", [P, T], I32)
         w1_raw = alloc("w1_raw", [P, PACK, H], F32)
         gn_sb = alloc("gn_sb", [P, PACK], F32)
         zero = alloc("zero", [P, 1], F32)
         one_half = alloc("one_half", [P, 1], F32)
         xs_rows = alloc("xs_rows", [P, T // 4], I32)
-        scale_rows = [slice(32 * q, 32 * q + 4) for q in range(4)]
-        for q, rows in enumerate(scale_rows):
-            (nc.scalar, nc.sync)[q % 2].dma_start(xs_rows[rows, :], x_scales[0, 4 * q : 4 * q + 4, :].bitcast(I32))
+        nc.scalar.dma_start(xs_rows[:SCALE_ROWS, :], x_scales[0].bitcast(I32))
         nc.scalar.dma_start(gn_sb[:], gn.rearrange("(p t) o -> p (t o)", t=PACK))
         nc.sync.dma_start(offs_sb[:], offs)
         nc.sync.dma_start(w1_raw[:], w1.rearrange("(p j) c -> p j c", j=PACK))
         nc.sync.dma_start(xw_win[:], x_words[0].rearrange("p n t -> p (n t)").bitcast(I32))
         for lst, src in zip(lists, (p1, p2, p3)):
             nc.sync.dma_start(lst[:], src)
-        w2_raw = [alloc("w2_raw%d" % h, [P, PACK, N // 2], F32) for h in range(2)]
-        for h in range(2):
-            nc.sync.dma_start(w2_raw[h][:], w2.rearrange("(p j) c -> p j c", j=PACK)[:, :, h * (N // 2) : (h + 1) * (N // 2)])
 
         nc.gpsimd.memset(zero[:], 0.0)
         nc.scalar.activation(one_half[:], zero[:], ACT.Sigmoid)
@@ -81,10 +83,17 @@ def tile_picked_isingm_none_p_kernel(tc, x_words, x_scales, w1, gn, w2, offs, p1
         make_identity(nc, ident[:])
 
         nc.vector.memset(xs_win[:].bitcast(I32), 0)
-        for rows in scale_rows:
-            nc.vector.tensor_copy(xs_win[rows, :].bitcast(I32), xs_rows[rows, :])
+        nc.vector.tensor_copy(xs_win[:SCALE_ROWS, :].bitcast(I32), xs_rows[:SCALE_ROWS, :])
+        xs_picked = alloc("xs_picked", [P, S], U8)
+        nc.vector.tensor_copy(xs_picked[:], xs_win[:].indirect(offs_sb[:]))
         xs = alloc("xs", [P, S], U8)
-        nc.vector.tensor_copy(xs[:], xs_win[:].indirect(offs_sb[:]))
+        nc.vector.memset(xs[:].bitcast(I32), 0)
+        nc.vector.tensor_copy(xs[0:4, :].bitcast(I32), xs_picked[0:4, :].bitcast(I32))
+        for q in range(1, 4):
+            nc.sync.dma_start(xs[32 * q : 32 * q + 4, :].bitcast(I32), xs_picked[4 * q : 4 * q + 4, :].bitcast(I32))
+        w2_raw = [place("w2_raw%d" % h, [P, PACK, N // 2], F32, W2_SECOND + (h - 1) * W2_HALF_BYTES) for h in range(2)]
+        for h in range(2):
+            nc.sync.dma_start(w2_raw[h][:], w2.rearrange("(p j) c -> p j c", j=PACK)[:, :, h * (N // 2) : (h + 1) * (N // 2)])
 
         w1_bf = alloc("w1_bf", [P, PACK, P, PACK], BF16)
         w1_src = w1_raw[:].rearrange("p j (m t) -> p m j t", t=PACK)
@@ -115,7 +124,7 @@ def tile_picked_isingm_none_p_kernel(tc, x_words, x_scales, w1, gn, w2, offs, p1
         y = {t: alloc("y%d" % t, [P, S], F32) for t in VECTOR_TILES}
         a2 = {t: alloc("a2_%d" % t, [P, S], F32) for t in SCALAR_TILES}
         y_turned = alloc("y_turned", [P, 2, S // P, P], F32)
-        gy_y1 = alloc("gy_y1", [P, PACK + 2, S], F32, "w2_raw0")
+        gy_y1 = place("gy_y1", [P, PACK + 2, S], F32, 0)
         gy = gy_y1[:, :PACK]
         a2_turned, y_back = {}, {}
 

@@ -67,7 +67,7 @@ def tile_picked_isingm_none_p_kernel(tc, x_words, x_scales, w1, gn, w2, offs, p1
         w1_raw = alloc("w1_raw", [P, PACK, H], F32)
         gn_sb = alloc("gn_sb", [P, PACK], F32)
         zero = alloc("zero", [P, 1], F32)
-        one_half = alloc("one_half", [P, 1], F32)
+        no_bias = alloc("no_bias", [P, 1], F32)
         xs_rows = alloc("xs_rows", [P, T // 4], I32)
         nc.scalar.dma_start(xs_rows[:SCALE_ROWS, :], x_scales[0].bitcast(I32))
         nc.scalar.dma_start(gn_sb[:], gn.rearrange("(p t) o -> p (t o)", t=PACK))
@@ -78,7 +78,7 @@ def tile_picked_isingm_none_p_kernel(tc, x_words, x_scales, w1, gn, w2, offs, p1
             nc.sync.dma_start(lst[:], src)
 
         nc.gpsimd.memset(zero[:], 0.0)
-        nc.scalar.activation(one_half[:], zero[:], ACT.Sigmoid)
+        nc.scalar.activation(no_bias[:], zero[:], ACT.Tanh)
         ident = alloc("ident", [P, P], F32)
         make_identity(nc, ident[:])
 
@@ -121,38 +121,26 @@ def tile_picked_isingm_none_p_kernel(tc, x_words, x_scales, w1, gn, w2, offs, p1
             dst, cols = a_parts[t][h]
             product(dst[:], w1_codes, w1_scales, t, xw[:, cols], xs[:, cols])
 
-        y = {t: alloc("y%d" % t, [P, S], F32) for t in VECTOR_TILES}
-        a2 = {t: alloc("a2_%d" % t, [P, S], F32) for t in SCALAR_TILES}
+        y = [alloc("y%d" % t, [P, S], F32) for t in range(PACK)]
         y_turned = alloc("y_turned", [P, 2, S // P, P], F32)
         gy_y1 = place("gy_y1", [P, PACK + 2, S], F32, 0)
         gy = gy_y1[:, :PACK]
-        a2_turned, y_back = {}, {}
+        y_bank = {}
 
         def make_y(t, part):
             src, cols = a_parts[t][part]
-            nc.scalar.activation(y[t][:, cols], src[:], ACT.Tanh)
+            nc.scalar.activation(y[t][:, cols], src[:], ACT.Tanh, bias=no_bias[:, 0:1])
 
-        def make_a2(t, part):
-            src, cols = a_parts[t][part]
-            nc.scalar.activation(a2[t][:, cols], src[:], ACT.Copy, scale=2.0)
-
-        def turn_a2(t):
-            a2_turned[t] = bank("a2_turned%d" % t, [P, S // P, P], 6 + t // 2)
+        def turn_y(t):
+            y_bank[t] = bank("y_bank%d" % t, [P, S // P, P], 6 + t // 2)
             for jb in range(S // P):
-                nc.tensor.transpose(a2_turned[t][:, jb, :], a2[t][:, jb * P : (jb + 1) * P], ident[:])
+                nc.tensor.transpose(y_bank[t][:, jb, :], y[t][:, jb * P : (jb + 1) * P], ident[:])
 
-        def make_y_turned(t):
-            nc.scalar.activation(y_turned[:, t // 2], a2_turned[t][:], ACT.Tanh, scale=one_half[:, 0:1])
-            y_back[t] = bank("y_back%d" % t, [P, S // P, P], 4 + t // 2)
-            for jb in range(S // P):
-                nc.tensor.transpose(y_back[t][:, jb, :], y_turned[:, t // 2, jb, :], ident[:])
+        def keep_turned_y(t):
+            nc.scalar.copy(y_turned[:, t // 2], y_bank[t][:])
 
         def make_gy(t):
-            gain = gn_sb[:, t : t + 1]
-            if t in VECTOR_TILES:
-                nc.vector.tensor_scalar(gy[:, t, :], y[t][:], gain, None, ALU.mult)
-            else:
-                nc.scalar.activation(gy[:, t, :], y_back[t][:].rearrange("p k j -> p (k j)"), ACT.Copy, scale=gain)
+            nc.vector.tensor_scalar(gy[:, t, :], y[t][:], gn_sb[:, t : t + 1], None, ALU.mult)
 
         def entries(r, j0, n):
             return lists[r][:, j0 // GROUP : (j0 + n) // GROUP]
@@ -197,7 +185,7 @@ def tile_picked_isingm_none_p_kernel(tc, x_words, x_scales, w1, gn, w2, offs, p1
         def fetch_and_add(c, tiles, t, dsts):
             j0, n = CHUNKS[c]
             for r in range(LISTS):
-                nc.scalar.activation(dsts[r], a2[t][:].indirect(entries(r, j0, n)), ACT.Sigmoid)
+                nc.scalar.activation(dsts[r], y[t][:].indirect(entries(r, j0, n)), ACT.Copy)
             for jb in range(n // P):
                 for r in range(LISTS):
                     nc.tensor.matmul(
@@ -212,12 +200,10 @@ def tile_picked_isingm_none_p_kernel(tc, x_words, x_scales, w1, gn, w2, offs, p1
         def make_half_u(c, tiles, number):
             j0, n = CHUNKS[c]
             turned = alloc("half_u_turned%d_%d" % (c, tiles[0]), [P, len(tiles), n], F32)
-            nc.vector.scalar_tensor_tensor(
+            nc.vector.tensor_tensor(
                 turned[:],
                 sums[c, tiles][:].rearrange("j b k p -> j b (k p)"),
-                -LISTS / 2,
                 y_turned[:, own_tiles(tiles), j0 // P : (j0 + n) // P, :].rearrange("j b k p -> j b (k p)"),
-                ALU.add,
                 ALU.mult,
             )
             half_u[c, tiles] = bank("half_u%d_%d" % (c, tiles[0]), [P, len(tiles), n], number)
@@ -227,7 +213,7 @@ def tile_picked_isingm_none_p_kernel(tc, x_words, x_scales, w1, gn, w2, offs, p1
 
         def tanh_of_half_u(c, tiles):
             j0, n = CHUNKS[c]
-            nc.scalar.activation(tanh_u[:, feature_tiles(tiles), j0 : j0 + n], half_u[c, tiles][:], ACT.Tanh, scale=2.0)
+            nc.scalar.activation(tanh_u[:, feature_tiles(tiles), j0 : j0 + n], half_u[c, tiles][:], ACT.Tanh)
 
         z_bf, z_codes, z_scales = {}, {}, {}
 
@@ -279,13 +265,13 @@ def tile_picked_isingm_none_p_kernel(tc, x_words, x_scales, w1, gn, w2, offs, p1
         cast_w2(nc.vector.tensor_copy, 0, slice(0, N // 2))
         for h in range(2):
             make_y(0, h)
-            make_a2(1, h)
-        turn_a2(1)
+            make_y(1, h)
+        turn_y(1)
         make_y(2, 0)
         open_sums(0, SCALAR_TILES, 0)
         fetch_and_add(0, SCALAR_TILES, 1, [s_first[:, 0, r, :] for r in range(LISTS)])
-        make_a2(3, 0)
-        turn_a2(3)
+        make_y(3, 0)
+        turn_y(3)
         fetch_first(0, halves[0])
         fetch_second(0, 0, y12_first[:, 0, :])
         make_gy(0)
@@ -297,24 +283,23 @@ def tile_picked_isingm_none_p_kernel(tc, x_words, x_scales, w1, gn, w2, offs, p1
         fetch_third(0, 2)
         make_gy(2)
         make_u(0, 2)
-        make_y_turned(1)
+        keep_turned_y(1)
         fetch_and_add(0, SCALAR_TILES, 3, [s_first[:, 1, r, :] for r in range(LISTS)])
-        make_y_turned(3)
+        keep_turned_y(3)
         for t in VECTOR_TILES:
             fetch_first(t, halves[1])
+        for t in SCALAR_TILES:
+            make_gy(t)
         make_half_u(0, SCALAR_TILES, 1)
 
         open_sums(1, SCALAR_TILES, 0)
         fetch_and_add(1, SCALAR_TILES, 1, [s_second[:, r, :] for r in range(LISTS)])
         tanh_of_u(0, VECTOR_TILES)
-        for t in SCALAR_TILES:
-            make_gy(t)
+        w2_bf[1] = alloc("w2_bf1", [P, N // 2, PACK], BF16)
+        cast_w2(nc.scalar.copy, 1, slice(0, N // 2))
         tanh_of_half_u(0, SCALAR_TILES)
         s_late = alloc("s_late", [P, 2 + 2 * LISTS, P], F32, "half_u_turned0_1")
         fetch_and_add(1, SCALAR_TILES, 3, [s_second[:, LISTS, :], s_late[:, 0, :], s_late[:, 1, :]])
-        w2_bf[1] = alloc("w2_bf1", [P, N // 2, PACK], BF16)
-        cast_w2(nc.vector.tensor_copy, 1, slice(0, N // 2))
-        quantise_w2(1)
         fetch_second(1, 0, s_first[:, 1, LISTS - 1, P:])
         fetch_second(1, 2, s_first[:, 1, LISTS - 1, :P])
         for t in VECTOR_TILES:
@@ -325,6 +310,7 @@ def tile_picked_isingm_none_p_kernel(tc, x_words, x_scales, w1, gn, w2, offs, p1
         for t in VECTOR_TILES:
             make_u(1, t)
         make_z(0, z_first[:])
+        quantise_w2(1)
         make_half_u(1, SCALAR_TILES, 3)
         open_sums(LAST, (3,), 0)
         fetch_and_add(LAST, (3,), 3, [s_late[:, 2 + LISTS + r, :] for r in range(LISTS)])

@@ -21,15 +21,13 @@ PACK = 4
 GROUP = 16
 LISTS = 3
 HALF = S // 2
-CHUNKS = ((0, 256), (256, 128), (384, 128))
-LAST = len(CHUNKS) - 1
+BLOCKS = S // P
 VECTOR_TILES = (0, 2)
 SCALAR_TILES = (1, 3)
 W1_VECTOR = 64
 RUN = 4
 SCALE_ROWS = K // 32
 W2_HALF_BYTES = PACK * (N // 2) * 4
-W2_SECOND = (PACK + 2) * S * 4
 
 
 def tile_picked_isingm_none_p_kernel(tc, x_words, x_scales, w1, gn, w2, offs, p1, p2, p3, out):
@@ -62,7 +60,7 @@ def tile_picked_isingm_none_p_kernel(tc, x_words, x_scales, w1, gn, w2, offs, p1
 
         offs_sb = sb.tile([P, S // GROUP], U16, name="offs_sb")
         lists = [sb.tile([P, S // GROUP], U16, name="list%d" % r) for r in range(LISTS)]
-        xs_win = place("xs_win", [P, T], U8, W2_SECOND - T // 2)
+        xs_win = place("xs_win", [P, T], U8, W2_HALF_BYTES - T // 2)
         xw_win = alloc("xw_win", [P, T], I32)
         w1_raw = alloc("w1_raw", [P, PACK, H], F32)
         gn_sb = alloc("gn_sb", [P, PACK], F32)
@@ -91,7 +89,7 @@ def tile_picked_isingm_none_p_kernel(tc, x_words, x_scales, w1, gn, w2, offs, p1
         nc.vector.tensor_copy(xs[0:4, :].bitcast(I32), xs_picked[0:4, :].bitcast(I32))
         for q in range(1, 4):
             nc.sync.dma_start(xs[32 * q : 32 * q + 4, :].bitcast(I32), xs_picked[4 * q : 4 * q + 4, :].bitcast(I32))
-        w2_raw = [place("w2_raw%d" % h, [P, PACK, N // 2], F32, W2_SECOND + (h - 1) * W2_HALF_BYTES) for h in range(2)]
+        w2_raw = [place("w2_raw%d" % h, [P, PACK, N // 2], F32, h * W2_HALF_BYTES) for h in range(2)]
         for h in range(2):
             nc.sync.dma_start(w2_raw[h][:], w2.rearrange("(p j) c -> p j c", j=PACK)[:, :, h * (N // 2) : (h + 1) * (N // 2)])
 
@@ -122,221 +120,183 @@ def tile_picked_isingm_none_p_kernel(tc, x_words, x_scales, w1, gn, w2, offs, p1
             product(dst[:], w1_codes, w1_scales, t, xw[:, cols], xs[:, cols])
 
         y = [alloc("y%d" % t, [P, S], F32) for t in range(PACK)]
-        y_turned = alloc("y_turned", [P, 2, S // P, P], F32)
-        gy_y1 = place("gy_y1", [P, PACK + 2, S], F32, 0)
-        gy = gy_y1[:, :PACK]
-        y_bank = {}
+        y_turned = alloc("y_turned", [P, BLOCKS, PACK, P], F32)
+        gy = alloc("gy", [P, PACK, S], F32)
+        tanh_u = alloc("tanh_u", [P, PACK, S], F32)
+
+        def columns(block, count=1):
+            return slice(block * P, (block + count) * P)
+
+        def entries(r, block, count=1):
+            return lists[r][:, block * P // GROUP : (block + count) * P // GROUP]
+
+        def every_second(tiles):
+            return slice(tiles[0], tiles[-1] + 1, 2)
 
         def make_y(t, part):
             src, cols = a_parts[t][part]
             nc.scalar.activation(y[t][:, cols], src[:], ACT.Tanh, bias=no_bias[:, 0:1])
 
-        def turn_y(t):
-            y_bank[t] = bank("y_bank%d" % t, [P, S // P, P], 6 + t // 2)
-            for jb in range(S // P):
-                nc.tensor.transpose(y_bank[t][:, jb, :], y[t][:, jb * P : (jb + 1) * P], ident[:])
+        def turn_y(t, dst):
+            for jb in range(dst.shape[1]):
+                nc.tensor.transpose(dst[:, jb, :], y[t][:, columns(jb)], ident[:])
 
-        def keep_turned_y(t):
-            nc.scalar.copy(y_turned[:, t // 2], y_bank[t][:])
+        def make_gy_on_gpsimd(t):
+            nc.gpsimd.tensor_scalar(gy[:, t, :], y[t][:], gn_sb[:, t : t + 1], 0.0, ALU.mult, ALU.add)
 
-        def make_gy(t):
-            nc.vector.tensor_scalar(gy[:, t, :], y[t][:], gn_sb[:, t : t + 1], None, ALU.mult)
+        def fetch(t, r, dst, block, count, on_vector):
+            looked_up = y[t][:].indirect(entries(r, block, count))
+            if on_vector:
+                nc.vector.tensor_copy(dst, looked_up)
+            else:
+                nc.scalar.activation(dst, looked_up, ACT.Copy)
 
-        def entries(r, j0, n):
-            return lists[r][:, j0 // GROUP : (j0 + n) // GROUP]
-
-        def feature_tiles(tiles):
-            return slice(tiles[0], tiles[-1] + 1, 2)
-
-        def own_tiles(tiles):
-            return slice(tiles[0] // 2, tiles[-1] // 2 + 1)
-
-        y1 = gy_y1[:, PACK:]
-        fl = alloc("fl", [P, 2, S], F32)
-        y12 = {}
-        u = alloc("u", [P, 2, S], F32)
-        tanh_u = alloc("tanh_u", [P, PACK, S], F32)
-
-        def fetch_first(t, cols):
-            nc.vector.tensor_copy(y1[:, t // 2, cols], y[t][:].indirect(entries(0, cols.start, cols.stop - cols.start)))
-
-        def fetch_second(c, t, dst):
-            j0, n = CHUNKS[c]
-            y12[c, t] = dst
-            nc.vector.tensor_tensor(dst, y[t][:].indirect(entries(1, j0, n)), y1[:, t // 2, j0 : j0 + n], ALU.add)
-
-        def fetch_third(c, t):
-            j0, n = CHUNKS[c]
-            nc.vector.tensor_tensor(fl[:, t // 2, j0 : j0 + n], y[t][:].indirect(entries(2, j0, n)), y12[c, t], ALU.add)
-
-        def make_u(c, t):
-            j0, n = CHUNKS[c]
-            nc.vector.tensor_tensor(u[:, t // 2, j0 : j0 + n], fl[:, t // 2, j0 : j0 + n], y[t][:, j0 : j0 + n], ALU.mult)
-
-        def tanh_of_u(c, tiles):
-            j0, n = CHUNKS[c]
-            nc.scalar.activation(tanh_u[:, feature_tiles(tiles), j0 : j0 + n], u[:, own_tiles(tiles), j0 : j0 + n], ACT.Tanh)
-
-        sums, half_u = {}, {}
-
-        def open_sums(c, tiles, number):
-            sums[c, tiles] = bank("sums%d_%d" % (c, tiles[0]), [P, len(tiles), CHUNKS[c][1] // P, P], number)
-
-        def fetch_and_add(c, tiles, t, dsts):
-            j0, n = CHUNKS[c]
+        def fetch_and_sum(t, dsts, block, sums):
             for r in range(LISTS):
-                nc.scalar.activation(dsts[r], y[t][:].indirect(entries(r, j0, n)), ACT.Copy)
-            for jb in range(n // P):
-                for r in range(LISTS):
-                    nc.tensor.matmul(
-                        sums[c, tiles][:, tiles.index(t), jb, :],
-                        dsts[r][:, jb * P : (jb + 1) * P],
-                        ident[:],
-                        start=(r == 0),
-                        stop=(r == LISTS - 1),
-                        is_transpose=True,
-                    )
+                fetch(t, r, dsts[r], block, len(sums), t in VECTOR_TILES)
+                for b, total in enumerate(sums):
+                    nc.tensor.matmul(total, dsts[r][:, columns(b)], ident[:], start=(r == 0), stop=(r == LISTS - 1), is_transpose=True)
 
-        def make_half_u(c, tiles, number):
-            j0, n = CHUNKS[c]
-            turned = alloc("half_u_turned%d_%d" % (c, tiles[0]), [P, len(tiles), n], F32)
-            nc.vector.tensor_tensor(
-                turned[:],
-                sums[c, tiles][:].rearrange("j b k p -> j b (k p)"),
-                y_turned[:, own_tiles(tiles), j0 // P : (j0 + n) // P, :].rearrange("j b k p -> j b (k p)"),
-                ALU.mult,
-            )
-            half_u[c, tiles] = bank("half_u%d_%d" % (c, tiles[0]), [P, len(tiles), n], number)
-            for b in range(len(tiles)):
-                for jb in range(n // P):
-                    nc.tensor.transpose(half_u[c, tiles][:, b, jb * P : (jb + 1) * P], turned[:, b, jb * P : (jb + 1) * P], ident[:])
+        def fetch_adding(t, r, dst, other, block, count):
+            nc.vector.tensor_tensor(dst, y[t][:].indirect(entries(r, block, count)), other, ALU.add)
 
-        def tanh_of_half_u(c, tiles):
-            j0, n = CHUNKS[c]
-            nc.scalar.activation(tanh_u[:, feature_tiles(tiles), j0 : j0 + n], half_u[c, tiles][:], ACT.Tanh)
+        def turned_product(name, sums, block, tiles, number):
+            count = sums.shape[1]
+            turned = alloc(name, [P, count, P], F32)
+            nc.vector.tensor_tensor(turned[:], sums, y_turned[:, block, tiles, :], ALU.mult)
+            back = bank(name + "_back", [P, count, P], number)
+            for b in range(count):
+                nc.tensor.transpose(back[:, b, :], turned[:, b, :], ident[:])
+            return back, turned
 
-        z_bf, z_codes, z_scales = {}, {}, {}
+        def make_tanh(src, tiles, block):
+            nc.scalar.activation(tanh_u[:, tiles, columns(block)], src, ACT.Tanh)
 
-        def make_z(c, dst):
-            j0, n = CHUNKS[c]
-            z_bf[c] = dst
+        def make_z(dst, block):
             nc.vector.tensor_tensor(
                 dst.rearrange("p (g i t) -> p g t i", i=RUN, t=PACK),
-                tanh_u[:, :, j0 : j0 + n].rearrange("p t (g i) -> p g t i", i=RUN),
-                gy[:, :, j0 : j0 + n].rearrange("p t (g i) -> p g t i", i=RUN),
+                tanh_u[:, :, columns(block)].rearrange("p t (g i) -> p g t i", i=RUN),
+                gy[:, :, columns(block)].rearrange("p t (g i) -> p g t i", i=RUN),
                 ALU.mult,
             )
 
-        def quantise_z(c):
-            n = CHUNKS[c][1]
-            z_codes[c] = alloc("z_codes%d" % c, [P, n], U32)
-            z_scales[c] = alloc("z_scales%d" % c, [P, n], U8)
-            nc.vector.quantize_mx(z_codes[c][:].bitcast(FP8X4), z_scales[c][:], z_bf[c])
+        def quantise_z(name, src):
+            n = src.shape[1] // PACK
+            codes = alloc(name + "_codes", [P, n], U32)
+            scales = alloc(name + "_scales", [P, n], U8)
+            nc.vector.quantize_mx(codes[:].bitcast(FP8X4), scales[:], src)
+            return codes, scales
 
-        w2_bf = {}
-        w2_codes = alloc("w2_codes", [P, N], U32)
+        w2_bf = alloc("w2_bf", [P, N, PACK], BF16)
         w2_scales = alloc("w2_scales", [P, N], U8)
-
-        def cast_w2(copy, h, cols):
-            copy(w2_bf[h][:, cols, :].rearrange("p (g i) t -> p g t i", i=RUN), w2_raw[h][:, :, cols].rearrange("p t (g i) -> p g t i", i=RUN))
-
-        def quantise_w2(h):
-            cols = slice(h * (N // 2), (h + 1) * (N // 2))
-            nc.vector.quantize_mx(w2_codes[:, cols].bitcast(FP8X4), w2_scales[:, cols], w2_bf[h][:].rearrange("p n t -> p (n t)"))
-
         out_rows = out.rearrange("(m p) j -> p m j", p=P)
 
-        def product_out(c, m0, count, number, copy, queue, tag=None):
-            j0, n = CHUNKS[c]
-            acc = bank("acc%d_%d" % (c, m0), [P, count, n], number)
+        def product_out(z, block, m0, count, number, copy, queue, tag=None):
+            n = z[0].shape[1]
+            acc = bank("acc%d_%d" % (block, m0), [P, count, n], number)
             for m in range(count):
-                product(acc[:, m, :], w2_codes, w2_scales, m0 + m, z_codes[c][:], z_scales[c][:])
-            res = alloc("res%d_%d" % (c, m0), [P, count, n], F32, tag)
+                product(acc[:, m, :], w2_codes, w2_scales, m0 + m, z[0][:], z[1][:])
+            res = alloc("res%d_%d" % (block, m0), [P, count, n], F32, tag)
             copy(res[:], acc[:])
-            queue.dma_start(out_rows[:, m0 : m0 + count, j0 : j0 + n], res[:])
+            queue.dma_start(out_rows[:, m0 : m0 + count, block * P : block * P + n], res[:])
 
-        s_first = alloc("s_first", [P, 2, LISTS, HALF], F32)
-        s_second = alloc("s_second", [P, LISTS + 1, P], F32)
-        y12_first = alloc("y12_first", [P, 2, HALF], F32)
-        z_first = alloc("z_first", [P, HALF * PACK], BF16)
-        z_last = alloc("z_last", [P, P * PACK], BF16)
-
-        w2_bf[0] = alloc("w2_bf0", [P, N // 2, PACK], BF16)
-        cast_w2(nc.vector.tensor_copy, 0, slice(0, N // 2))
+        nc.vector.tensor_copy(
+            w2_bf[:, : N // 2, :].rearrange("p (g i) t -> p g t i", i=RUN), w2_raw[0][:].rearrange("p t (g i) -> p g t i", i=RUN)
+        )
+        nc.gpsimd.tensor_scalar(w2_bf[:, N // 2 :, :], w2_raw[1][:].rearrange("p t n -> p n t"), 1.0, 0.0, ALU.mult, ALU.add)
+        early0 = place("early0", [P, LISTS + 1, HALF], F32, 0)
+        early = {t: alloc("early%d" % t, [P, LISTS, HALF], F32) for t in range(1, PACK)}
+        early[0] = early0
+        first_late2 = alloc("first_late2", [P, HALF], F32)
+        first_late = {0: early0[:, LISTS, :], 2: first_late2[:]}
         for h in range(2):
             make_y(0, h)
             make_y(1, h)
-        turn_y(1)
         make_y(2, 0)
-        open_sums(0, SCALAR_TILES, 0)
-        fetch_and_add(0, SCALAR_TILES, 1, [s_first[:, 0, r, :] for r in range(LISTS)])
+        turned_banks = {t: bank("turned%d" % t, [P, BLOCKS, P], 6 + t // 2) for t in SCALAR_TILES}
+        turned_pair = bank("turned_pair", [P, 2, 2, P], 0)
+        sums = [bank("sums%d" % jb, [P, PACK, P], 1 + jb) for jb in range(2)]
+
+        def early_chunk(t):
+            fetch_and_sum(t, [early[t][:, r, :] for r in range(LISTS)], 0, [total[:, t, :] for total in sums])
+
+        for t in range(PACK - 1):
+            make_gy_on_gpsimd(t)
+        early_chunk(0)
+        fetch(0, 0, first_late[0], 2, 2, True)
+        turn_y(1, turned_banks[1])
+        early_chunk(1)
+        for t in VECTOR_TILES:
+            turn_y(t, turned_pair[:, t // 2])
         make_y(3, 0)
-        turn_y(3)
-        fetch_first(0, halves[0])
-        fetch_second(0, 0, y12_first[:, 0, :])
-        make_gy(0)
-        fetch_third(0, 0)
-        fetch_first(2, halves[0])
-        make_u(0, 0)
-        fetch_second(0, 2, y12_first[:, 1, :])
-        quantise_w2(0)
-        fetch_third(0, 2)
-        make_gy(2)
-        make_u(0, 2)
-        keep_turned_y(1)
-        fetch_and_add(0, SCALAR_TILES, 3, [s_first[:, 1, r, :] for r in range(LISTS)])
-        keep_turned_y(3)
-        for t in VECTOR_TILES:
-            fetch_first(t, halves[1])
-        for t in SCALAR_TILES:
-            make_gy(t)
-        make_half_u(0, SCALAR_TILES, 1)
+        make_gy_on_gpsimd(3)
+        turn_y(3, turned_banks[3])
+        early_chunk(2)
+        fetch(2, 0, first_late[2], 2, 2, True)
+        nc.vector.tensor_copy(y_turned[:, :2, every_second(VECTOR_TILES), :], turned_pair[:].rearrange("j t b p -> j b t p"))
+        nc.scalar.copy(y_turned[:, :, 1, :], turned_banks[1][:])
+        early_chunk(3)
+        nc.scalar.copy(y_turned[:, :, 3, :], turned_banks[3][:])
 
-        open_sums(1, SCALAR_TILES, 0)
-        fetch_and_add(1, SCALAR_TILES, 1, [s_second[:, r, :] for r in range(LISTS)])
-        tanh_of_u(0, VECTOR_TILES)
-        w2_bf[1] = alloc("w2_bf1", [P, N // 2, PACK], BF16)
-        cast_w2(nc.scalar.copy, 1, slice(0, N // 2))
-        tanh_of_half_u(0, SCALAR_TILES)
-        s_late = alloc("s_late", [P, 2 + 2 * LISTS, P], F32, "half_u_turned0_1")
-        fetch_and_add(1, SCALAR_TILES, 3, [s_second[:, LISTS, :], s_late[:, 0, :], s_late[:, 1, :]])
-        fetch_second(1, 0, s_first[:, 1, LISTS - 1, P:])
-        fetch_second(1, 2, s_first[:, 1, LISTS - 1, :P])
-        for t in VECTOR_TILES:
-            fetch_third(1, t)
+        w2_codes = alloc("w2_codes", [P, N], U32)
+        fl = alloc("fl", [P, 2, HALF], F32)
+        u = alloc("u", [P, 2, HALF], F32)
 
-        open_sums(LAST, (1,), 6)
-        fetch_and_add(LAST, (1,), 1, [s_late[:, 2 + r, :] for r in range(LISTS)])
-        for t in VECTOR_TILES:
-            make_u(1, t)
-        make_z(0, z_first[:])
-        quantise_w2(1)
-        make_half_u(1, SCALAR_TILES, 3)
-        open_sums(LAST, (3,), 0)
-        fetch_and_add(LAST, (3,), 3, [s_late[:, 2 + LISTS + r, :] for r in range(LISTS)])
-        quantise_z(0)
-        tanh_of_u(1, VECTOR_TILES)
-        tanh_of_half_u(1, SCALAR_TILES)
-        for t in VECTOR_TILES:
-            fetch_second(LAST, t, s_late[:, t // 2, :])
-        for t in VECTOR_TILES:
-            fetch_third(LAST, t)
-        make_half_u(LAST, (1,), 7)
-        make_half_u(LAST, (3,), 1)
-        for t in VECTOR_TILES:
-            make_u(LAST, t)
-        tanh_of_half_u(LAST, (1,))
-        for t in VECTOR_TILES:
-            tanh_of_u(LAST, (t,))
-        tanh_of_half_u(LAST, (3,))
+        def second(t, block, dst, count=1):
+            fetch_adding(t, 1, dst, first_late[t][:, columns(block - 2, count)], block, count)
 
-        product_out(0, 0, 2, 4, nc.scalar.copy, nc.sync)
-        product_out(0, 2, 2, 5, nc.scalar.copy, nc.sync, "u")
-        make_z(1, s_late[:, 0:2, :].rearrange("p k j -> p (k j)").bitcast(BF16))
-        quantise_z(1)
-        product_out(1, 0, 2, 0, nc.scalar.copy, nc.sync)
-        product_out(1, 2, 2, 2, nc.scalar.copy, nc.sync)
-        make_z(LAST, z_last[:])
-        quantise_z(LAST)
-        for m, number in enumerate((3, 6, 7, 1)):
-            product_out(LAST, m, 1, number, (nc.vector.tensor_copy, nc.scalar.copy)[m % 2], nc.scalar if m == PACK - 1 else nc.sync)
+        def third(t, block, src, count=1):
+            fetch_adding(t, 2, fl[:, t // 2, columns(block - 2, count)], src, block, count)
+
+        def make_u(t, block, count=1):
+            cols = columns(block - 2, count)
+            nc.vector.tensor_tensor(u[:, t // 2, cols], fl[:, t // 2, cols], y[t][:, columns(block, count)], ALU.mult)
+
+        nc.vector.quantize_mx(w2_codes[:].bitcast(FP8X4), w2_scales[:], w2_bf[:].rearrange("p n t -> p (n t)"))
+        back0, turned0 = turned_product("u0", sums[0][:], 0, slice(0, PACK), 3)
+        back1, turned1 = turned_product("u1", sums[1][:], 1, slice(0, PACK), 4)
+
+        late = early[2][:].rearrange("p r (b j) -> p (r b) j", j=P)
+        sums2 = bank("sums2", [P, 2, P], 1)
+        fetch_and_sum(1, [late[:, r, :] for r in range(LISTS)], 2, [sums2[:, 0, :]])
+        fetch_and_sum(3, [late[:, LISTS + r, :] for r in range(LISTS)], 2, [sums2[:, 1, :]])
+        make_tanh(back0[:], slice(0, PACK), 0)
+        make_tanh(back1[:], slice(0, PACK), 1)
+        z_first = alloc("z_first", [P, HALF * PACK], BF16)
+        y12 = y_turned[:, 0].rearrange("j t p -> j (t p)")
+        second(0, 2, y12[:, :HALF], 2)
+        second(2, 2, y12[:, columns(2)])
+        third(0, 2, y12[:, :HALF], 2)
+        third(2, 2, y12[:, columns(2)])
+        make_z(z_first[:, : P * PACK], 0)
+        make_u(0, 2, 2)
+        make_u(2, 2)
+        make_z(z_first[:, P * PACK :], 1)
+
+        sums3 = {1: bank("sums3_1", [P, 1, P], 6), 3: bank("sums3_3", [P, 1, P], 2)}
+        fetch_and_sum(1, [turned0[:, r, :] for r in range(LISTS)], 3, [sums3[1][:, 0, :]])
+        back2, turned2 = turned_product("u2", sums2[:], 2, every_second(SCALAR_TILES), 5)
+        fetch_and_sum(3, [turned1[:, r, :] for r in range(LISTS)], 3, [sums3[3][:, 0, :]])
+        second(2, 3, y_turned[:, 2, 1, :])
+        z0 = quantise_z("z0", z_first[:])
+        third(2, 3, y_turned[:, 2, 1, :])
+        make_tanh(u[:, :, :P], every_second(VECTOR_TILES), 2)
+        make_tanh(back2[:], every_second(SCALAR_TILES), 2)
+        back3 = {t: turned_product("u3_%d" % t, sums3[t][:], 3, slice(t, t + 1), number)[0] for t, number in ((1, 7), (3, 0))}
+        make_u(2, 3)
+        make_tanh(back3[1][:], slice(1, 2), 3)
+        make_tanh(u[:, :, P:], every_second(VECTOR_TILES), 3)
+        make_tanh(back3[3][:], slice(3, 4), 3)
+
+        product_out(z0, 0, 0, 2, 3, nc.scalar.copy, nc.sync)
+        product_out(z0, 0, 2, 2, 4, nc.scalar.copy, nc.sync, "u")
+        z_second = turned1[:, 0:2, :].rearrange("p k j -> p (k j)").bitcast(BF16)
+        make_z(z_second, 2)
+        z2 = quantise_z("z2", z_second)
+        product_out(z2, 2, 0, 2, 1, nc.scalar.copy, nc.sync)
+        product_out(z2, 2, 2, 2, 2, nc.scalar.copy, nc.sync)
+        z_last = alloc("z_last", [P, P * PACK], BF16)
+        make_z(z_last[:], 3)
+        z3 = quantise_z("z3", z_last[:])
+        for m, number in enumerate((5, 6, 7, 0)):
+            product_out(z3, 3, m, 1, number, (nc.vector.tensor_copy, nc.scalar.copy)[m % 2], nc.scalar if m == PACK - 1 else nc.sync)

@@ -275,11 +275,11 @@ def tile_picked_isingm_none_p_kernel(tc, x_words, x_scales, w1, gn, w2, offs, p1
 
         sums3 = {1: bank("sums3_1", [P, 1, P], 6), 3: bank("sums3_3", [P, 1, P], 2)}
         fetch_and_sum(1, [turned0[:, r, :] for r in range(LISTS)], 3, [sums3[1][:, 0, :]])
-        back2, turned2 = turned_product("u2", sums2[:], 2, every_second(SCALAR_TILES), 5)
+        back2 = turned_product("u2", sums2[:], 2, every_second(SCALAR_TILES), 5)[0]
         fetch_and_sum(3, [turned1[:, r, :] for r in range(LISTS)], 3, [sums3[3][:, 0, :]])
-        second(2, 3, y_turned[:, 2, 1, :])
+        second(2, 3, tanh_u[:, 0, :P])
         z0 = quantise_z("z0", z_first[:])
-        third(2, 3, y_turned[:, 2, 1, :])
+        third(2, 3, tanh_u[:, 0, :P])
         make_tanh(u[:, :, :P], every_second(VECTOR_TILES), 2)
         make_tanh(back2[:], every_second(SCALAR_TILES), 2)
         back3 = {t: turned_product("u3_%d" % t, sums3[t][:], 3, slice(t, t + 1), number)[0] for t, number in ((1, 7), (3, 0))}
@@ -289,12 +289,12 @@ def tile_picked_isingm_none_p_kernel(tc, x_words, x_scales, w1, gn, w2, offs, p1
         make_tanh(back3[3][:], slice(3, 4), 3)
 
         product_out(z0, 0, 0, 2, 3, nc.scalar.copy, nc.sync)
-        product_out(z0, 0, 2, 2, 4, nc.scalar.copy, nc.sync, "u")
+        product_out(z0, 0, 2, 2, 2, nc.scalar.copy, nc.sync, "u")
         z_second = turned1[:, 0:2, :].rearrange("p k j -> p (k j)").bitcast(BF16)
         make_z(z_second, 2)
         z2 = quantise_z("z2", z_second)
         product_out(z2, 2, 0, 2, 1, nc.scalar.copy, nc.sync)
-        product_out(z2, 2, 2, 2, 2, nc.scalar.copy, nc.sync)
+        product_out(z2, 2, 2, 2, 4, nc.scalar.copy, nc.sync)
         z_last = alloc("z_last", [P, P * PACK], BF16)
         make_z(z_last[:], 3)
         z3 = quantise_z("z3", z_last[:])

@@ -64,7 +64,7 @@ def tile_picked_isingm_none_p_kernel(tc, x_words, x_scales, w1, gn, w2, offs, p1
         xw_win = alloc("xw_win", [P, T], I32)
         w1_raw = alloc("w1_raw", [P, PACK, H], F32)
         gn_sb = alloc("gn_sb", [P, PACK], F32)
-        zero = alloc("zero", [P, 1], F32)
+        zero = place("zero", [P, 1], F32, 2 * W2_HALF_BYTES)
         no_bias = alloc("no_bias", [P, 1], F32)
         xs_rows = alloc("xs_rows", [P, T // 4], I32)
         nc.scalar.dma_start(xs_rows[:SCALE_ROWS, :], x_scales[0].bitcast(I32))
@@ -142,7 +142,7 @@ def tile_picked_isingm_none_p_kernel(tc, x_words, x_scales, w1, gn, w2, offs, p1
                 nc.tensor.transpose(dst[:, jb, :], y[t][:, columns(jb)], ident[:])
 
         def make_gy_on_gpsimd(t):
-            nc.gpsimd.tensor_scalar(gy[:, t, :], y[t][:], gn_sb[:, t : t + 1], 0.0, ALU.mult, ALU.add)
+            nc.gpsimd.tensor_scalar(gy[:, t, :], y[t][:], gn_sb[:, t : t + 1], zero[:, 0:1], ALU.mult, ALU.add)
 
         def fetch(t, r, dst, block, count, on_vector):
             looked_up = y[t][:].indirect(entries(r, block, count))
@@ -231,10 +231,10 @@ def tile_picked_isingm_none_p_kernel(tc, x_words, x_scales, w1, gn, w2, offs, p1
         make_y(3, 0)
         make_gy_on_gpsimd(3)
         turn_y(3, turned_banks[3])
-        early_chunk(2)
-        fetch(2, 0, first_late[2], 2, 2, True)
-        nc.vector.tensor_copy(y_turned[:, :2, every_second(VECTOR_TILES), :], turned_pair[:].rearrange("j t b p -> j b t p"))
         nc.scalar.copy(y_turned[:, :, 1, :], turned_banks[1][:])
+        early_chunk(2)
+        fetch(2, 0, first_late[2][:, :P], 2, 1, True)
+        nc.vector.tensor_copy(y_turned[:, :2, every_second(VECTOR_TILES), :], turned_pair[:].rearrange("j t b p -> j b t p"))
         early_chunk(3)
         nc.scalar.copy(y_turned[:, :, 3, :], turned_banks[3][:])
 
@@ -253,6 +253,8 @@ def tile_picked_isingm_none_p_kernel(tc, x_words, x_scales, w1, gn, w2, offs, p1
             nc.vector.tensor_tensor(u[:, t // 2, cols], fl[:, t // 2, cols], y[t][:, columns(block, count)], ALU.mult)
 
         nc.vector.quantize_mx(w2_codes[:].bitcast(FP8X4), w2_scales[:], w2_bf[:].rearrange("p n t -> p (n t)"))
+        y12 = place("y12", [P, HALF], F32, 2 * W2_HALF_BYTES)
+        second(0, 2, y12[:], 2)
         back0, turned0 = turned_product("u0", sums[0][:], 0, slice(0, PACK), 3)
         back1, turned1 = turned_product("u1", sums[1][:], 1, slice(0, PACK), 4)
 
@@ -262,14 +264,13 @@ def tile_picked_isingm_none_p_kernel(tc, x_words, x_scales, w1, gn, w2, offs, p1
         fetch_and_sum(3, [late[:, LISTS + r, :] for r in range(LISTS)], 2, [sums2[:, 1, :]])
         make_tanh(back0[:], slice(0, PACK), 0)
         make_tanh(back1[:], slice(0, PACK), 1)
+        fetch(2, 0, turned0[:, LISTS, :], 3, 1, False)
         z_first = alloc("z_first", [P, HALF * PACK], BF16)
-        y12 = y_turned[:, 0].rearrange("j t p -> j (t p)")
-        second(0, 2, y12[:, :HALF], 2)
-        second(2, 2, y12[:, columns(2)])
-        third(0, 2, y12[:, :HALF], 2)
-        third(2, 2, y12[:, columns(2)])
+        second(2, 2, y_turned[:, 0, 0, :])
+        fetch_adding(0, 2, y_turned[:, 0, 2:, :].rearrange("j t p -> j (t p)"), y12[:], 2, 2)
+        third(2, 2, y_turned[:, 0, 0, :])
         make_z(z_first[:, : P * PACK], 0)
-        make_u(0, 2, 2)
+        nc.vector.tensor_tensor(u[:, 0, :], y_turned[:, 0, 2:, :].rearrange("j t p -> j (t p)"), y[0][:, HALF:], ALU.mult)
         make_u(2, 2)
         make_z(z_first[:, P * PACK :], 1)
 
@@ -277,7 +278,7 @@ def tile_picked_isingm_none_p_kernel(tc, x_words, x_scales, w1, gn, w2, offs, p1
         fetch_and_sum(1, [turned0[:, r, :] for r in range(LISTS)], 3, [sums3[1][:, 0, :]])
         back2 = turned_product("u2", sums2[:], 2, every_second(SCALAR_TILES), 5)[0]
         fetch_and_sum(3, [turned1[:, r, :] for r in range(LISTS)], 3, [sums3[3][:, 0, :]])
-        second(2, 3, tanh_u[:, 0, :P])
+        fetch_adding(2, 1, tanh_u[:, 0, :P], turned0[:, LISTS, :], 3, 1)
         z0 = quantise_z("z0", z_first[:])
         third(2, 3, tanh_u[:, 0, :P])
         make_tanh(u[:, :, :P], every_second(VECTOR_TILES), 2)

@@ -118,6 +118,9 @@ def tile_picked_isingm_none_p_kernel(tc, x_words, x_scales, w1, gn, w2, offs, p1
         for t, h in ((0, 0), (1, 0), (0, 1), (1, 1), (2, 0), (3, 0)):
             dst, cols = a_parts[t][h]
             product(dst[:], w1_codes, w1_scales, t, xw[:, cols], xs[:, cols])
+        a_turned = [bank("a_turned%d" % jb, [P, H], 6 + jb) for jb in range(2)]
+        for jb in range(2):
+            product(a_turned[jb][:], xw, xs, jb, w1_codes[:], w1_scales[:])
 
         y = [alloc("y%d" % t, [P, S], F32) for t in range(PACK)]
         y_turned = alloc("y_turned", [P, BLOCKS, PACK, P], F32)
@@ -139,7 +142,10 @@ def tile_picked_isingm_none_p_kernel(tc, x_words, x_scales, w1, gn, w2, offs, p1
 
         def turn_y(t, dst):
             for jb in range(dst.shape[1]):
-                nc.tensor.transpose(dst[:, jb, :], y[t][:, columns(jb)], ident[:])
+                nc.tensor.transpose(dst[:, jb, :], y[t][:, columns(2 + jb)], ident[:])
+
+        def make_turned_y(jb):
+            nc.scalar.activation(y_turned[:, jb].rearrange("j t p -> j (t p)"), a_turned[jb][:], ACT.Tanh, bias=no_bias[:, 0:1])
 
         def make_gy_on_gpsimd(t):
             nc.gpsimd.tensor_scalar(gy[:, t, :], y[t][:], gn_sb[:, t : t + 1], zero[:, 0:1], ALU.mult, ALU.add)
@@ -213,7 +219,6 @@ def tile_picked_isingm_none_p_kernel(tc, x_words, x_scales, w1, gn, w2, offs, p1
             make_y(0, h)
             make_y(1, h)
         make_y(2, 0)
-        turned_banks = {t: bank("turned%d" % t, [P, BLOCKS, P], 6 + t // 2) for t in SCALAR_TILES}
         turned_pair = bank("turned_pair", [P, 2, 2, P], 0)
         sums = [bank("sums%d" % jb, [P, PACK, P], 1 + jb) for jb in range(2)]
 
@@ -224,19 +229,17 @@ def tile_picked_isingm_none_p_kernel(tc, x_words, x_scales, w1, gn, w2, offs, p1
             make_gy_on_gpsimd(t)
         early_chunk(0)
         fetch(0, 0, first_late[0], 2, 2, True)
-        turn_y(1, turned_banks[1])
         early_chunk(1)
-        for t in VECTOR_TILES:
-            turn_y(t, turned_pair[:, t // 2])
         make_y(3, 0)
         make_gy_on_gpsimd(3)
-        turn_y(3, turned_banks[3])
-        nc.scalar.copy(y_turned[:, :, 1, :], turned_banks[1][:])
+        for t in SCALAR_TILES:
+            turn_y(t, turned_pair[:, t // 2])
+        make_turned_y(0)
         early_chunk(2)
         fetch(2, 0, first_late[2][:, :P], 2, 1, True)
-        nc.vector.tensor_copy(y_turned[:, :2, every_second(VECTOR_TILES), :], turned_pair[:].rearrange("j t b p -> j b t p"))
+        nc.vector.tensor_copy(y_turned[:, 2:, every_second(SCALAR_TILES), :], turned_pair[:].rearrange("j t b p -> j b t p"))
         early_chunk(3)
-        nc.scalar.copy(y_turned[:, :, 3, :], turned_banks[3][:])
+        make_turned_y(1)
 
         w2_codes = alloc("w2_codes", [P, N], U32)
         fl = alloc("fl", [P, 2, HALF], F32)

from contextlib import ExitStack

import concourse.mybir as mybir
from concourse.masks import make_identity

K, T, S, N, H = 512, 2048, 512, 512, 512
FLOPS = 2 * K * H * S + 2 * H * N * S

F32 = mybir.dt.float32
BF16 = mybir.dt.bfloat16
I32 = mybir.dt.int32
U32 = mybir.dt.uint32
U16 = mybir.dt.uint16
U8 = mybir.dt.uint8
FP8X4 = mybir.dt.float8_e4m3fn_x4
ALU = mybir.AluOpType
ACT = mybir.ActivationFunctionType

P = 128
PACK = 4
GROUP = 16
LISTS = 3
HALF = S // 2
BLOCKS = S // P
VECTOR_TILES = (0, 2)
SCALAR_TILES = (1, 3)
W1_VECTOR = 64
RUN = 4
SCALE_ROWS = K // 32
W2_HALF_BYTES = PACK * (N // 2) * 4


def tile_picked_isingm_none_p_kernel(tc, x_words, x_scales, w1, gn, w2, offs, p1, p2, p3, out):
    nc = tc.nc
    with ExitStack() as ctx:
        sb = ctx.enter_context(tc.tile_pool(name="sb", bufs=1))
        shared = ctx.enter_context(tc.tile_pool(name="shared", bufs=1))
        ps = ctx.enter_context(tc.psum_pool(name="ps", bufs=1))

        def alloc(name, shape, dtype, tag=None):
            return sb.tile(shape, dtype, name=name, tag=tag or name, align_bytes=64)

        def place(name, shape, dtype, offset):
            return shared.tile(shape, dtype, name=name, align_bytes=64, offset=offset)

        def bank(name, shape, number):
            return ps.tile(shape, F32, name=name, tag="bank%d" % number)

        def product(dst, w_codes, w_scales, tile, codes, scales):
            cols = slice(tile * P, (tile + 1) * P)
            nc.tensor.matmul_mx(
                out=dst,
                lhsT=w_codes[:, cols].bitcast(FP8X4),
                lhsT_scale=w_scales[:, cols],
                rhs=codes.bitcast(FP8X4),
                rhs_scale=scales,
                start=True,
                stop=True,
            )

        offs_sb = sb.tile([P, S // GROUP], U16, name="offs_sb")
        lists = [sb.tile([P, S // GROUP], U16, name="list%d" % r) for r in range(LISTS)]
        xs_win = place("xs_win", [P, T], U8, W2_HALF_BYTES - T // 2)
        xw_win = alloc("xw_win", [P, T], I32)
        w1_raw = alloc("w1_raw", [P, PACK, H], F32)
        gn_sb = alloc("gn_sb", [P, PACK], F32)
        zero = place("zero", [P, 1], F32, 2 * W2_HALF_BYTES)
        no_bias = alloc("no_bias", [P, 1], F32)
        xs_rows = alloc("xs_rows", [P, T // 4], I32)
        nc.scalar.dma_start(xs_rows[:SCALE_ROWS, :], x_scales[0].bitcast(I32))
        nc.scalar.dma_start(gn_sb[:], gn.rearrange("(p t) o -> p (t o)", t=PACK))
        nc.sync.dma_start(offs_sb[:], offs)
        nc.sync.dma_start(w1_raw[:], w1.rearrange("(p j) c -> p j c", j=PACK))
        nc.sync.dma_start(xw_win[:], x_words[0].rearrange("p n t -> p (n t)").bitcast(I32))
        for lst, src in zip(lists, (p1, p2, p3)):
            nc.sync.dma_start(lst[:], src)

        nc.gpsimd.memset(zero[:], 0.0)
        nc.scalar.activation(no_bias[:], zero[:], ACT.Tanh)
        ident = alloc("ident", [P, P], F32)
        make_identity(nc, ident[:])

        nc.vector.memset(xs_win[:].bitcast(I32), 0)
        nc.vector.tensor_copy(xs_win[:SCALE_ROWS, :].bitcast(I32), xs_rows[:SCALE_ROWS, :])
        xs_picked = alloc("xs_picked", [P, S], U8)
        nc.vector.tensor_copy(xs_picked[:], xs_win[:].indirect(offs_sb[:]))
        xs = alloc("xs", [P, S], U8)
        nc.vector.memset(xs[:].bitcast(I32), 0)
        nc.vector.tensor_copy(xs[0:4, :].bitcast(I32), xs_picked[0:4, :].bitcast(I32))
        for q in range(1, 4):
            nc.sync.dma_start(xs[32 * q : 32 * q + 4, :].bitcast(I32), xs_picked[4 * q : 4 * q + 4, :].bitcast(I32))
        w2_raw = [place("w2_raw%d" % h, [P, PACK, N // 2], F32, h * W2_HALF_BYTES) for h in range(2)]
        for h in range(2):
            nc.sync.dma_start(w2_raw[h][:], w2.rearrange("(p j) c -> p j c", j=PACK)[:, :, h * (N // 2) : (h + 1) * (N // 2)])

        w1_bf = alloc("w1_bf", [P, PACK, P, PACK], BF16)
        w1_src = w1_raw[:].rearrange("p j (m t) -> p m j t", t=PACK)
        w1_dst = w1_bf[:].rearrange("p t m j -> p m j t")
        nc.vector.tensor_copy(w1_dst[:, :W1_VECTOR], w1_src[:, :W1_VECTOR])
        nc.scalar.copy(w1_dst[:, W1_VECTOR:], w1_src[:, W1_VECTOR:])
        w1_codes = alloc("w1_codes", [P, H], U32)
        w1_scales = alloc("w1_scales", [P, H], U8)

        def quantise_w1(t0):
            cols = slice(t0 * P, (t0 + 2) * P)
            nc.vector.quantize_mx(w1_codes[:, cols].bitcast(FP8X4), w1_scales[:, cols], w1_bf[:, t0 : t0 + 2].rearrange("p t m j -> p (t m j)"))

        quantise_w1(0)

        halves = [slice(h * HALF, (h + 1) * HALF) for h in range(2)]
        a_parts = {t: [(bank("a%d%d" % (t, h), [P, HALF], 2 * t + h), halves[h]) for h in range(2)] for t in range(2)}
        for t in range(2, PACK):
            a_parts[t] = [(bank("a%d" % t, [P, S], t + 2), slice(0, S))]
        xw = alloc("xw", [P, S], U32)
        for cols in halves:
            nc.vector.tensor_copy(xw[:, cols], xw_win[:].bitcast(U32).indirect(offs_sb[:, cols.start // GROUP : cols.stop // GROUP]))
        quantise_w1(2)
        for t, h in ((0, 0), (1, 0), (0, 1), (1, 1), (2, 0), (3, 0)):
            dst, cols = a_parts[t][h]
            product(dst[:], w1_codes, w1_scales, t, xw[:, cols], xs[:, cols])
        a_turned = [bank("a_turned%d" % jb, [P, H], 6 + jb) for jb in range(2)]
        for jb in range(2):
            product(a_turned[jb][:], xw, xs, jb, w1_codes[:], w1_scales[:])

        y = [alloc("y%d" % t, [P, S], F32) for t in range(PACK)]
        y_turned = alloc("y_turned", [P, BLOCKS, PACK, P], F32)
        gy = alloc("gy", [P, PACK, S], F32)
        tanh_u = alloc("tanh_u", [P, PACK, S], F32)

        def columns(block, count=1):
            return slice(block * P, (block + count) * P)

        def entries(r, block, count=1):
            return lists[r][:, block * P // GROUP : (block + count) * P // GROUP]

        def every_second(tiles):
            return slice(tiles[0], tiles[-1] + 1, 2)

        def make_y(t, part):
            src, cols = a_parts[t][part]
            nc.scalar.activation(y[t][:, cols], src[:], ACT.Tanh, bias=no_bias[:, 0:1])

        def turn_y(t, dst):
            for jb in range(dst.shape[1]):
                nc.tensor.transpose(dst[:, jb, :], y[t][:, columns(2 + jb)], ident[:])

        def make_turned_y(jb):
            nc.scalar.activation(y_turned[:, jb].rearrange("j t p -> j (t p)"), a_turned[jb][:], ACT.Tanh, bias=no_bias[:, 0:1])

        def make_gy_on_gpsimd(t):
            nc.gpsimd.tensor_scalar(gy[:, t, :], y[t][:], gn_sb[:, t : t + 1], zero[:, 0:1], ALU.mult, ALU.add)

        def fetch(t, r, dst, block, count, on_vector):
            looked_up = y[t][:].indirect(entries(r, block, count))
            if on_vector:
                nc.vector.tensor_copy(dst, looked_up)
            else:
                nc.scalar.activation(dst, looked_up, ACT.Copy)

        def fetch_and_sum(t, dsts, block, sums):
            for r in range(LISTS):
                fetch(t, r, dsts[r], block, len(sums), t in VECTOR_TILES)
                for b, total in enumerate(sums):
                    nc.tensor.matmul(total, dsts[r][:, columns(b)], ident[:], start=(r == 0), stop=(r == LISTS - 1), is_transpose=True)

        def fetch_adding(t, r, dst, other, block, count):
            nc.vector.tensor_tensor(dst, y[t][:].indirect(entries(r, block, count)), other, ALU.add)

        def turned_product(name, sums, block, tiles, number):
            count = sums.shape[1]
            turned = alloc(name, [P, count, P], F32)
            nc.vector.tensor_tensor(turned[:], sums, y_turned[:, block, tiles, :], ALU.mult)
            back = bank(name + "_back", [P, count, P], number)
            for b in range(count):
                nc.tensor.transpose(back[:, b, :], turned[:, b, :], ident[:])
            return back, turned

        def make_tanh(src, tiles, block):
            nc.scalar.activation(tanh_u[:, tiles, columns(block)], src, ACT.Tanh)

        def make_z(dst, block):
            nc.vector.tensor_tensor(
                dst.rearrange("p (g i t) -> p g t i", i=RUN, t=PACK),
                tanh_u[:, :, columns(block)].rearrange("p t (g i) -> p g t i", i=RUN),
                gy[:, :, columns(block)].rearrange("p t (g i) -> p g t i", i=RUN),
                ALU.mult,
            )

        def quantise_z(name, src):
            n = src.shape[1] // PACK
            codes = alloc(name + "_codes", [P, n], U32)
            scales = alloc(name + "_scales", [P, n], U8)
            nc.vector.quantize_mx(codes[:].bitcast(FP8X4), scales[:], src)
            return codes, scales

        w2_bf = alloc("w2_bf", [P, N, PACK], BF16)
        w2_scales = alloc("w2_scales", [P, N], U8)
        out_rows = out.rearrange("(m p) j -> p m j", p=P)

        def product_out(z, block, m0, count, number, copy, queue, tag=None):
            n = z[0].shape[1]
            acc = bank("acc%d_%d" % (block, m0), [P, count, n], number)
            for m in range(count):
                product(acc[:, m, :], w2_codes, w2_scales, m0 + m, z[0][:], z[1][:])
            res = alloc("res%d_%d" % (block, m0), [P, count, n], F32, tag)
            copy(res[:], acc[:])
            queue.dma_start(out_rows[:, m0 : m0 + count, block * P : block * P + n], res[:])

        nc.vector.tensor_copy(
            w2_bf[:, : N // 2, :].rearrange("p (g i) t -> p g t i", i=RUN), w2_raw[0][:].rearrange("p t (g i) -> p g t i", i=RUN)
        )
        nc.gpsimd.tensor_scalar(w2_bf[:, N // 2 :, :], w2_raw[1][:].rearrange("p t n -> p n t"), 1.0, 0.0, ALU.mult, ALU.add)
        early0 = place("early0", [P, LISTS + 1, HALF], F32, 0)
        early = {t: alloc("early%d" % t, [P, LISTS, HALF], F32) for t in range(1, PACK)}
        early[0] = early0
        first_late2 = alloc("first_late2", [P, HALF], F32)
        first_late = {0: early0[:, LISTS, :], 2: first_late2[:]}
        for h in range(2):
            make_y(0, h)
            make_y(1, h)
        make_y(2, 0)
        turned_pair = bank("turned_pair", [P, 2, 2, P], 0)
        sums = [bank("sums%d" % jb, [P, PACK, P], 1 + jb) for jb in range(2)]

        def early_chunk(t):
            fetch_and_sum(t, [early[t][:, r, :] for r in range(LISTS)], 0, [total[:, t, :] for total in sums])

        for t in range(PACK - 1):
            make_gy_on_gpsimd(t)
        early_chunk(0)
        fetch(0, 0, first_late[0], 2, 2, True)
        early_chunk(1)
        make_y(3, 0)
        make_gy_on_gpsimd(3)
        for t in SCALAR_TILES:
            turn_y(t, turned_pair[:, t // 2])
        make_turned_y(0)
        early_chunk(2)
        fetch(2, 0, first_late[2][:, :P], 2, 1, True)
        nc.vector.tensor_copy(y_turned[:, 2:, every_second(SCALAR_TILES), :], turned_pair[:].rearrange("j t b p -> j b t p"))
        early_chunk(3)
        make_turned_y(1)

        w2_codes = alloc("w2_codes", [P, N], U32)
        fl = alloc("fl", [P, 2, HALF], F32)
        u = alloc("u", [P, 2, HALF], F32)

        def second(t, block, dst, count=1):
            fetch_adding(t, 1, dst, first_late[t][:, columns(block - 2, count)], block, count)

        def third(t, block, src, count=1):
            fetch_adding(t, 2, fl[:, t // 2, columns(block - 2, count)], src, block, count)

        def make_u(t, block, count=1):
            cols = columns(block - 2, count)
            nc.vector.tensor_tensor(u[:, t // 2, cols], fl[:, t // 2, cols], y[t][:, columns(block, count)], ALU.mult)

        nc.vector.quantize_mx(w2_codes[:].bitcast(FP8X4), w2_scales[:], w2_bf[:].rearrange("p n t -> p (n t)"))
        y12 = place("y12", [P, HALF], F32, 2 * W2_HALF_BYTES)
        second(0, 2, y12[:], 2)
        back0, turned0 = turned_product("u0", sums[0][:], 0, slice(0, PACK), 3)
        back1, turned1 = turned_product("u1", sums[1][:], 1, slice(0, PACK), 4)

        late = early[2][:].rearrange("p r (b j) -> p (r b) j", j=P)
        sums2 = bank("sums2", [P, 2, P], 1)
        fetch_and_sum(1, [late[:, r, :] for r in range(LISTS)], 2, [sums2[:, 0, :]])
        fetch_and_sum(3, [late[:, LISTS + r, :] for r in range(LISTS)], 2, [sums2[:, 1, :]])
        make_tanh(back0[:], slice(0, PACK), 0)
        make_tanh(back1[:], slice(0, PACK), 1)
        fetch(2, 0, turned0[:, LISTS, :], 3, 1, False)
        z_first = alloc("z_first", [P, HALF * PACK], BF16)
        second(2, 2, y_turned[:, 0, 0, :])
        fetch_adding(0, 2, y_turned[:, 0, 2:, :].rearrange("j t p -> j (t p)"), y12[:], 2, 2)
        third(2, 2, y_turned[:, 0, 0, :])
        make_z(z_first[:, : P * PACK], 0)
        nc.vector.tensor_tensor(u[:, 0, :], y_turned[:, 0, 2:, :].rearrange("j t p -> j (t p)"), y[0][:, HALF:], ALU.mult)
        make_u(2, 2)
        make_z(z_first[:, P * PACK :], 1)

        sums3 = {1: bank("sums3_1", [P, 1, P], 6), 3: bank("sums3_3", [P, 1, P], 2)}
        fetch_and_sum(1, [turned0[:, r, :] for r in range(LISTS)], 3, [sums3[1][:, 0, :]])
        back2 = turned_product("u2", sums2[:], 2, every_second(SCALAR_TILES), 5)[0]
        fetch_and_sum(3, [turned1[:, r, :] for r in range(LISTS)], 3, [sums3[3][:, 0, :]])
        fetch_adding(2, 1, tanh_u[:, 0, :P], turned0[:, LISTS, :], 3, 1)
        z0 = quantise_z("z0", z_first[:])
        third(2, 3, tanh_u[:, 0, :P])
        make_tanh(u[:, :, :P], every_second(VECTOR_TILES), 2)
        make_tanh(back2[:], every_second(SCALAR_TILES), 2)
        back3 = {t: turned_product("u3_%d" % t, sums3[t][:], 3, slice(t, t + 1), number)[0] for t, number in ((1, 7), (3, 0))}
        make_u(2, 3)
        make_tanh(back3[1][:], slice(1, 2), 3)
        make_tanh(u[:, :, P:], every_second(VECTOR_TILES), 3)
        make_tanh(back3[3][:], slice(3, 4), 3)

        product_out(z0, 0, 0, 2, 3, nc.scalar.copy, nc.sync)
        product_out(z0, 0, 2, 2, 2, nc.scalar.copy, nc.sync, "u")
        z_second = turned1[:, 0:2, :].rearrange("p k j -> p (k j)").bitcast(BF16)
        make_z(z_second, 2)
        z2 = quantise_z("z2", z_second)
        product_out(z2, 2, 0, 2, 1, nc.scalar.copy, nc.sync)
        product_out(z2, 2, 2, 2, 4, nc.scalar.copy, nc.sync)
        z_last = alloc("z_last", [P, P * PACK], BF16)
        make_z(z_last[:], 3)
        z3 = quantise_z("z3", z_last[:])
        for m, number in enumerate((5, 6, 7, 0)):
            product_out(z3, 3, m, 1, number, (nc.vector.tensor_copy, nc.scalar.copy)[m % 2], nc.scalar if m == PACK - 1 else nc.sync)
